import numpy as np, ml_dtypes
CORES = [16,18,20,22]
N = 4
BF = ml_dtypes.bfloat16
def gentries(a):
    return np.ascontiguousarray(a.reshape(8, 16, -1).transpose(0, 2, 1)).reshape(8, -1)
def gtable(e):
    e = np.asarray(e); return np.ascontiguousarray(e.reshape(8, -1, 16).transpose(0, 2, 1)).reshape(128, -1).astype(np.int32)
C, K0, NQ, T, L, DS, SB = 4096, 128, 128, 3, 4, 1, 14
KM = K0 + T * NQ
def machine(rng, k, p, q):
    cl = rng.permutation(np.concatenate([np.arange(k), rng.integers(0, k, C - k)]))
    o = np.argsort(cl, kind="stable"); size = np.bincount(cl, minlength=k); first = np.add.accumulate(size) - size
    x = rng.integers(0, k, (16, k))[:, cl]; nx = o[first[x] + rng.integers(0, size[x])]
    out = rng.integers(0, 16, (16, k))[:, cl]
    out = np.where(rng.random((16, C)) < p, rng.integers(0, 16, (16, C)), out)
    nx = np.where(rng.random((16, C)) < q, rng.integers(0, C, (16, C)), nx)
    return nx, out, cl
def machines(rng):
    nx = np.empty((N, 8, 16, C), np.int64); out = np.empty((N, 8, 16, C), np.int64)
    for r in range(N):
        for g in range(8):
            p = float(rng.choice(np.array([0.004, 0.01, 0.03])))
            nx[r, g], out[r, g], cl = machine(rng, int(rng.choice(np.array([30, 80, 200, 500]))), p, 0.3 * p)
    return nx, out
def others(rng):
    return (rng.integers(0, C, (N, 8, K0)), rng.integers(0, 2 ** SB, (N, 8, T, NQ)), rng.integers(0, 16, (N, 8, T, NQ)),
            rng.integers(0, 16, (N, 8, 16, L)), rng.integers(0, 16, (N, 8, T, 16, L)))
def fresh(rng, ex):
    b = C // (T + 1); c = np.arange(C)
    nx = rng.integers(0, C, (16, C)); out = rng.integers(0, 16, (16, C)); nx[15] = c
    for d in range(3): out[d] = (c >> (4 * d)) & 15
    for t in range(T): nx[3 + t] = (t + 1) * b + rng.integers(0, b, C)
    ex[13:] = 15; ex[13:, L - 1] = np.arange(3)
    return nx, out, rng.integers(0, b, K0), np.repeat(3 + np.arange(T), NQ).reshape(T, NQ)
def pack(nx, out, bk, qs, qc, ex, zs):
    return {"mt": np.ascontiguousarray(np.roll((16 * nx + out).reshape(N, 128, C), DS, axis=0)).astype(np.int32),
            "bk": np.stack([gtable(a) for a in bk]), "qs": np.stack([gtable(a.reshape(8, -1)) for a in qs]), "qc": np.stack([gtable(a.reshape(8, -1)) for a in qc]),
            "ex": np.ascontiguousarray(ex.reshape(N, 128, L)).astype(np.int32), "zs": np.ascontiguousarray(zs.transpose(0, 1, 3, 2, 4)).reshape(N, 128, T * L).astype(np.int32)}
def setup_inputs(rng):
    nx, out = machines(rng)
    return pack(nx, out, *others(rng))
def setup_inputs_grow(rng):
    nx, out = machines(rng); bk, qs, qc, ex, zs = others(rng); c = np.arange(C); h = C // 2
    for r in range(N):
        o = rng.permutation(8)
        for g in o[:3]: nx[r, g], out[r, g], bk[r, g], qc[r, g] = fresh(rng, ex[r, g])
        g = o[2]; nx[r, g, 4:3 + T] = np.where(c >= C // (T + 1), c, nx[r, g, 4:3 + T])
        qs[r, g, 1:, :8] = 2 ** SB - 1 - np.arange(8) * (2 ** SB // (K0 + NQ))
        for g in o[3:6]:
            k = int(rng.integers(20, 61)); nx[r, g], out[r, g], cl = machine(rng, k, 0.0, 0.0)
            one = np.unique(cl, return_index=True)[1]
            bk[r, g] = rng.permutation(np.concatenate([one, rng.integers(0, C, K0 - k)]))
        g = o[5]
        nx[r, g, 15] = c; out[r, g, 15] = np.where(c < h, 3, 9); nx[r, g, 14, :h] = rng.integers(h, C, h)
        one = np.unique(cl[:h], return_index=True)[1]
        bk[r, g] = rng.permutation(np.concatenate([one, rng.integers(0, h, K0 - len(one))]))
        qc[r, g, 0] = 14; ex[r, g] = rng.integers(0, 14, (16, L)); zs[r, g, 0, int(rng.integers(1, 16))] = 15
    return pack(nx, out, bk, qs, qc, ex, zs)
def setup_inputs_near(rng):
    nx = np.empty((N, 8, 16, C), np.int64); out = np.empty((N, 8, 16, C), np.int64); bk, qs, qc, ex, zs = others(rng)
    for r in range(N):
        for g in range(8):
            x, y, cl = machine(rng, 40, 0.0, 0.0); y = np.minimum(np.maximum(y, 1), 14); x[15] = np.arange(C)
            c = np.flatnonzero(rng.random(C) < 0.5); a = rng.integers(0, 16, len(c)); b = (a + rng.integers(1, 16, len(c))) & 15
            y[a, c] += 1
            if (r + g) & 1: y[b, c] -= 1
            nx[r, g] = x; out[r, g] = y; ex[r, g] = 15; ex[r, g, :, L - 1] = rng.permutation(16)
    return pack(nx, out, bk, qs, qc, ex, zs)
def setup_inputs_alike(rng):
    nx, out = machines(rng); bk, qs, qc, ex, zs = others(rng)
    bk[:, ::2] = np.take_along_axis(rng.integers(0, C, (N, 4, 6)), rng.integers(0, 6, (N, 4, K0)), 2)
    zs = np.take_along_axis(zs, rng.integers(0, 5, (N, 8, T, 16))[..., None], 3)
    ex[:, 1::4] = np.repeat(ex[:, 1::4, :4], 4, axis=2)
    qs[:, 3] = rng.integers(0, 2 ** SB, 4)[rng.integers(0, 4, (N, T, NQ))]; qc[:, 3] = rng.integers(0, 16, 2)[rng.integers(0, 2, (N, T, NQ))]
    for r in range(N):
        nx[r, 5], out[r, 5], bk[r, 5], qc[r, 5] = fresh(rng, ex[r, 5])
        qs[r, 5] = rng.integers(0, 2 ** SB, 3)[rng.integers(0, 3, (T, NQ))]
    c = np.arange(C)
    nx[:, 7] = np.where(rng.random((N, 16, C)) < 0.1, 0, rng.integers(0, C, (N, 16, C))); nx[:, 7, 15] = c
    out[:, 7] = np.where((c == 0) | (c >= C // 2), 0, rng.integers(1, 16, (N, 16, C)))
    out[1::2, 7] = 15 - out[1::2, 7]
    bk[:, 7] = rng.integers(1, C // 2, (N, K0)); qc[:, 7] = rng.integers(0, 15, (N, T, NQ))
    ex[:, 7] = 15; ex[:, 7, :, L - 1] = np.argsort(rng.random((N, 16)), axis=-1)
    for r in range(N):
        if r & 2:
            nx[r, 7, 14] = np.where(rng.random(C) < 0.5, bk[r, 7][rng.integers(0, K0, C)], rng.integers(1, C // 2, C))
            qc[r, 7, 0] = 14; zs[r, 7, :, :, :L - 1] = 15
    return pack(nx, out, bk, qs, qc, ex, zs)
def setup_inputs_ends(rng):
    nx, out = machines(rng); bk, qs, qc, ex, zs = others(rng); e = np.array([0, C - 1]); l = np.array([0, 15])
    nx = np.where(rng.random(nx.shape) < 0.2, e[rng.integers(0, 2, nx.shape)], nx)
    qs[:, ::2] = np.array([0, 2 ** SB - 1])[rng.integers(0, 2, (N, 4, T, NQ))]
    qs[:, 1::2, 0] = (rng.integers(0, K0, (N, 4, NQ)) * (2 ** SB // K0) - rng.integers(0, 2, (N, 4, NQ))) & (2 ** SB - 1)
    qc[:, 1] = l[rng.integers(0, 2, (N, T, NQ))]; bk[:, 2] = e[rng.integers(0, 2, (N, K0))]; bk[:, :, 0] = 0; bk[:, :, K0 - 1] = C - 1
    ex[:, 4] = l[rng.integers(0, 2, (N, 16, L))]; zs[:, 4] = l[rng.integers(0, 2, (N, T, 16, L))]; ex[:, 5] = 15; zs[:, 7] = 0
    return pack(nx, out, bk, qs, qc, ex, zs)
def setup_inputs_spread(rng):
    a = rng.choice(np.array([1, 3, 8]), (N, 8, 1, 1)); b = rng.choice(np.array([1, 2, 6]), (N, 8, 1, 1))
    nx = (C * rng.random((N, 8, 16, C)) ** a).astype(np.int64); out = (16 * rng.random((N, 8, 16, C)) ** b).astype(np.int64)
    bk = (C * rng.random((N, 8, K0)) ** a[..., 0]).astype(np.int64); qs = (2 ** SB * rng.random((N, 8, T, NQ)) ** b).astype(np.int64)
    qc = (16 * rng.random((N, 8, T, NQ)) ** 2).astype(np.int64)
    ex = (16 * rng.random((N, 8, 16, L)) ** 2).astype(np.int64); zs = (16 * rng.random((N, 8, T, 16, L)) ** 2).astype(np.int64)
    return pack(nx, out, bk, qs, qc, ex, zs)
def check_inputs(d):
    bad = []
    for k, hi in (("mt", 16 * C - 1), ("bk", C - 1), ("qs", 2 ** SB - 1), ("qc", 15), ("ex", 15), ("zs", 15)):
        if np.min(d[k]) < 0 or np.max(d[k]) > hi: bad.append("range of " + k)
    return bad
def walk(tb, q, w):
    r = np.arange(N)[:, None, None, None]; g = np.arange(8)[None, :, None, None]; s = q[:, :, None, :]
    for i in range(L):
        v = tb[r, g, w[:, :, :, i][..., None], s]; s = v >> 4
    return v & 15
def reference(mt, bk, qs, qc, ex, zs):
    tb = np.roll(mt.astype(np.int64), -DS, axis=0).reshape(N, 8, 16, C)
    s_ = np.stack([gentries(a) for a in qs]).astype(np.int64).reshape(N, 8, T, NQ); c_ = np.stack([gentries(a) for a in qc]).astype(np.int64).reshape(N, 8, T, NQ)
    E = ex.astype(np.int64).reshape(N, 8, 16, L); Z = zs.astype(np.int64).reshape(N, 8, 16, T, L)
    kn = np.zeros((N, 8, KM), np.int64); rec = np.zeros((N, 8, 16, KM), np.int64); cnt = np.full((N, 8, 1), K0, np.int64)
    kn[:, :, :K0] = np.stack([gentries(a) for a in bk]); rec[..., :K0] = walk(tb, kn[:, :, :K0], E)
    r3 = np.arange(N)[:, None, None]; g3 = np.arange(8)[None, :, None]; ms = []
    for t in range(T):
        b = np.take_along_axis(kn, (s_[:, :, t] * cnt) >> SB, 2)
        q = tb[r3, g3, c_[:, :, t], b] >> 4
        rq = walk(tb, q, E)
        eq = np.broadcast_to((np.arange(KM) < cnt)[:, :, None, :], (N, 8, NQ, KM))
        for e in range(16): eq = eq & (rq[:, :, e, :, None] == rec[:, :, e, None, :])
        hit = np.any(eq, axis=3); new = (~hit).astype(np.int64)
        m = np.where(hit, np.argmax(eq, axis=3), cnt + np.add.accumulate(new, axis=2) - new)
        i, j, n = np.nonzero(new)
        kn[i, j, m[i, j, n]] = q[i, j, n]; rec[i, j, :, m[i, j, n]] = rq[i, j, :, n]
        cnt = cnt + np.add.reduce(new, axis=2)[..., None]; ms.append(m)
        zt = Z[:, :, :, t]
        differ = walk(tb, q, zt) != walk(tb, np.take_along_axis(kn, m, 2), zt)
        best = np.argmax(np.add.reduce(differ.astype(np.int64), axis=3), axis=2)
        E[:, :, t] = zt[r3[..., 0], g3[..., 0], best]
        rec[:, :, t] = walk(tb, kn, E[:, :, t:t + 1])[:, :, 0]
    rec = np.where((np.arange(KM) < cnt)[:, :, None, :], rec, -1)
    return {"ym": np.concatenate(ms, axis=2).astype(np.float32), "yr": rec.reshape(N, 128, KM).astype(np.float32), "ye": E.reshape(N, 128, L).astype(np.float32)}

@@ -1,0 +1,678 @@
+import numpy as np
+from concourse.mybir import AluOpType, AxisListType, ActivationFunctionType
+
+OP = AluOpType
+AF = ActivationFunctionType
+CWS = [1024, 1024, 1024, 512, 512]
+NCH = len(CWS)
+C27 = 201326592.0
+EPS = 0.499969482421875
+COSTS = [(0.00100, 1.5, 0.00042, 0.10), (0.00090, 1.2, 0.00042, 0.05), (0.00105, 1.9, 0.0006, 0.15)]
+TRIES = 1000
+SEED = 3
+NB = 3
+
+F, B, H, I, U = "float32", "bfloat16", "float16", "int32", "uint16"
+SCRATCH = {}
+for _n, _w, _d in [
+        ("mti", 4096, I), ("raw", 4096, I), ("wt", 4096, F), ("xw", 4096, F), ("ow", 4096, B),
+        ("wd", 16, I), ("bki", 8, I), ("qsi", 24, I), ("qci", 24, I), ("pi", 8, I), ("ix", 24, F),
+        ("qg", 128, F), ("qm", 128, F), ("pg", 128, F), ("c16", 16, F), ("io640", 640, F), ("c8", 8, F),
+        ("blk", 128, B), ("eqm", 128, B), ("i128", 128, B), ("jb", 128, B), ("jj", 2048, B), ("nj", 128, B),
+        ("blkp", 128, B), ("tmp", 128, B), ("tmp2", 128, B), ("tmb", 128, B), ("pmx", 128, B), ("blkpp", 128, B), ("blki", 128, B),
+        ("zb", 248, B), ("b8f", 16, F), ("keep", 384, B), ("cole", 16, F), ("nlneg", 8, H), ("npm", 8, F), ("cnp", 8, F),
+        ("neg1", 384, F), ("z8", 8, F), ("c15", 16, B), ("c15f", 16, F),
+        ("wdf", 24, F), ("dd", 512, B), ("wrb", 512, B), ("dm", 128, B), ("msk", 128, B),
+        ("sel", 12 * 2048, B), ("qcl", 24, U), ("lrow", 384, F), ("lm", 384, B), ("qsf", 24, F), ("bkl", 8, U),
+        ("ki", 8, I), ("kl", 8, U), ("qgt", 128, H), ("ql", 8, U), ("xi", 128, F), ("xl0", 128, U), ("xl1", 128, U), ("xk", 640, F),
+        ("y0", 2048, H), ("y1", 2048, H), ("y2", 2048, H),
+        ("g30", 1024, H), ("g31", 1024, H), ("g32", 1024, H), ("g33", 1024, H),
+        ("g40", 1024, B), ("g41", 1024, B), ("g42", 1024, B), ("g43", 1024, B),
+        ("l30", 128, U), ("l31", 128, U), ("l32", 128, U), ("lm3", 128, U),
+        ("l40", 128, U), ("l41", 128, U), ("l42", 128, U), ("l43", 128, U),
+        ("pz0", 512, F), ("pz1", 512, F), ("pz2", 512, F), ("pzn", 640, F), ("rr", 512, B), ("rn", 640, B), ("invn", 512, B),
+        ("r2", 384, B), ("rq2", 128, B), ("lhb", 1024, B),
+        ("sc", 3072, F), ("nn", 8, F), ("vl", 8, F), ("uu", 8, H), ("inc", 8, H), ("ww", 8, H), ("mn", 8, H), ("ml", 8, U), ("cnt", 4, H),
+        ("pl0", 8, U), ("pl1", 8, U), ("pl2", 8, U), ("num", 512, F), ("ymt", 384, F), ("inv", 128, B),
+        ("aq", 128, B), ("ne", 128, B), ("sm", 8, F), ("dd2", 16, B), ("oh", 4, F), ("ws", 4, B),
+        ("mk", 8, F), ("ya", 16, F), ("pw", 512, H), ("lw", 32, U), ("gw", 512, H), ("lw2", 32, U),
+        ("gz0", 512, B), ("gz1", 512, B), ("gz2", 512, B), ("yrt", 512, F)]:
+    SCRATCH[_n] = ("sbuf", [128, _w], _d)
+PSUM = ["pa0", "pa1", "pb0", "pb1", "pc0", "pc1", "pd0", "pe0"]
+for _n in PSUM:
+    SCRATCH[_n] = ("psum", [128, 512], F)
+SEMAPHORES = ["cv", "cs", "cp", "cg", "sent", "dex", "dzs", "dbk", "dqs", "dqc", "dym", "dyr", "dye"] + ["dmt%d" % h for h in range(NCH)] + ["arr%d" % h for h in range(NCH)]
+CSEM = {"V": "cv", "S": "cs", "P": "cp", "G": "cg"}
+PLAN = {}
+
+
+def cost(w, c):
+    return w[0] + c[0] * (w[1] + c[1] * w[2]) + c[2] * w[3]
+
+
+def evaluate(ops, order, c):
+    free, fin, end = {}, [0.0] * len(ops), 0.0
+    for i, q in order:
+        o = ops[i]
+        s = free.get(q, 0.0)
+        for d in o["deps"]:
+            s = max(s, fin[d] + c[3])
+        for d in o["soft"]:
+            if ops[d]["run"] != q:
+                s = max(s, fin[d] + c[3])
+        e = s + cost(o["alt"][q][1], c)
+        free[q] = e
+        fin[i] = e + o["lat"]
+        end = max(end, fin[i])
+    return end
+
+
+def place(ops, pre, succ, pr, al, durs, hop):
+    n = len(ops)
+    pr = list(pr)
+    for i in range(n - 1, -1, -1):
+        for s in succ[i]:
+            if pr[i] <= pr[s]:
+                pr[i] = pr[s] + 1e-6
+    line, fin, got = {}, [0.0] * n, []
+    for i in sorted(range(n), key=lambda x: -pr[x]):
+        o = ops[i]
+        best = None
+        for x, q in enumerate(o["alt"]):
+            if len(o["alt"]) > 1 and ((al[i] > 0.75 and x == 0) or (0.5 < al[i] <= 0.75 and x == 1)):
+                continue
+            t = 0.0
+            for d in pre[i]:
+                t = max(t, fin[d] + (0.0 if ops[d]["run"] == q and d in o["soft"] else ops[d]["lat"] + hop))
+            s, e = line.setdefault(q, ([], []))
+            w = durs[i][q]
+            k = len(s)
+            while k and e[k - 1] > t:
+                k -= 1
+            while k < len(s) and s[k] < max(t, e[k - 1] if k else 0.0) + w - 1e-9:
+                k += 1
+            t = max(t, e[k - 1] if k else 0.0)
+            if best is None or t + w < best[0]:
+                best = (t + w, t, q, k)
+        f, t, q, k = best
+        line[q][0].insert(k, t)
+        line[q][1].insert(k, f)
+        o["run"] = q
+        fin[i] = f
+        got.append((t, len(got), i, q))
+    got.sort()
+    return [(i, q) for _, _, i, q in got]
+
+
+def plan(ops):
+    n = len(ops)
+    c = COSTS[0]
+    durs = [{q: cost(o["alt"][q][1], c) for q in o["alt"]} for o in ops]
+    pre = [sorted(o["deps"] | o["soft"]) for o in ops]
+    succ = [[] for _ in range(n)]
+    for i in range(n):
+        for d in pre[i]:
+            succ[d].append(i)
+    prio = [0.0] * n
+    for i in range(n - 1, -1, -1):
+        prio[i] = min(durs[i].values()) + ops[i]["lat"] + max([prio[s] + c[3] for s in succ[i]] + [0.0])
+    rng = np.random.RandomState(SEED)
+    best, bp, bal = None, prio, [0.6] * n
+    for k in range(TRIES):
+        pr, al = bp, bal
+        if k:
+            amp = [0.5, 2.0, 6.0, 15.0][k % 4]
+            frac = [0.003, 0.01, 0.03, 0.1][(k // 4) % 4]
+            x, y, z = rng.rand(n).tolist(), rng.rand(n).tolist(), rng.rand(n).tolist()
+            pr = [bp[i] + (amp * (x[i] - 0.5) if y[i] < frac else 0.0) for i in range(n)]
+            al = [(0.45 + 0.4 * z[i] if y[i] < frac else bal[i]) for i in range(n)]
+        order = place(ops, pre, succ, pr, al, durs, c[3])
+        end = [evaluate(ops, order, x) for x in COSTS]
+        score = sum(e / (1.0 + j) for j, e in enumerate(end))
+        if best is None or score < best[0]:
+            best, bp, bal = (score, end, order), pr, al
+    return best
+
+
+def rank_program(g, core, T, topo):
+    rank = T.rank_of(core)
+    if rank is None:
+        return
+    queue = {"V": g.vector, "S": g.scalar, "P": g.tensor, "G": g, "Y": g.sync, "D": None}
+    ops = []
+    wrote, readers = {}, {}
+
+    def view(name, c0=0, c1=None, st=1):
+        if c1 is None:
+            c1 = SCRATCH[name][1][1]
+        ap = T[name][:, c0:c1] if st == 1 else T[name][:, c0:c1:st]
+        return (ap, name, c0, c1, (c1 - c0 + st - 1) // st)
+
+    def do(alt, reads, writes, free=False, tok=None, lat=0.0, dep=()):
+        i = len(ops)
+        deps, soft = set(dep), set()
+        for v in reads:
+            ps = v[1] in PSUM
+            for (a, b, j) in wrote.get(v[1], []):
+                if a < v[3] and v[2] < b:
+                    deps.add(j)
+                elif ps:
+                    soft.add(j)
+            if ps:
+                soft.update(j for (a, b, j) in readers.get(v[1], []))
+        for v in writes:
+            ps = v[1] in PSUM
+            for (a, b, j) in wrote.get(v[1], []):
+                if ps:
+                    soft.add(j)
+                elif a < v[3] and v[2] < b and not (free and ops[j]["free"]):
+                    deps.add(j)
+            for (a, b, j) in readers.get(v[1], []):
+                if a < v[3] and v[2] < b:
+                    deps.add(j)
+                elif ps:
+                    soft.add(j)
+        ops.append({"alt": alt, "lat": lat, "deps": deps, "soft": soft - deps, "tok": tok, "free": free, "run": None,
+                    "nm": writes[0][1] if writes else "-"})
+        for v in writes:
+            if not free:
+                for d in (wrote, readers):
+                    d[v[1]] = [r for r in d.get(v[1], []) if not (v[2] <= r[0] and r[1] <= v[3])]
+            wrote.setdefault(v[1], []).append((v[2], v[3], i))
+        for v in reads:
+            readers.setdefault(v[1], []).append((v[2], v[3], i))
+        return i
+
+    chains = {}
+
+    def chain(q, i):
+        if q in chains:
+            ops[i]["soft"].add(chains[q])
+        chains[q] = i
+
+    def flight(i, out, us, tok, lat):
+        j = do({"D": (None, (us, 0, 0, 0))}, [], out, tok=tok, lat=lat, dep=[i])
+        chain("D", j)
+
+    def dma(q, out, in_ap, sem, us):
+        i = do({q: (lambda e: e.dma_start(out[0], in_ap).then_inc(T.sem[sem], 16), (0.1, 0, 0, 0))}, [], [], tok=())
+        chain(q, i)
+        flight(i, [out], us, (sem, 16), 2.0)
+
+    def sca(s):
+        return [s] if isinstance(s, tuple) else []
+
+    def val(s):
+        return s[0] if isinstance(s, tuple) else s
+
+    def two(*vs):
+        return all(SCRATCH[v[1]][2] in (B, H, U) for v in vs)
+
+    def dv(n, half=False):
+        return (0.03, max(64, n * (0.5 if half else 1.0)), 0, 0)
+
+    def ind(v, idx):
+        return v[0] if idx is None else v[0].indirect(idx[0])
+
+    def lst(idx):
+        return [] if idx is None else [idx]
+
+    def a_ts(out, in0, s1, op0, s2=None, op1=None, idx=None):
+        i0 = ind(in0, idx)
+        w = dv(out[4], two(out, in0)) if idx is None else (0.05, 0, out[4], 0)
+        if op1 is None:
+            return (lambda e: e.tensor_scalar(out[0], i0, val(s1), None, op0), w)
+        return (lambda e: e.tensor_scalar(out[0], i0, val(s1), val(s2), op0, op1), w)
+
+    def a_act(out, in_, scale=1.0, bias=0.0, func=AF.Identity, idx=None):
+        i0 = ind(in_, idx)
+        return (lambda e: e.activation(out[0], i0, func, bias=val(bias), scale=val(scale)),
+                (0.065, 0, out[4], 0) if idx else (0.065, out[4], 0, 0))
+
+    def a_cp(out, in_, idx=None):
+        i0 = ind(in_, idx)
+        return (lambda e: e.tensor_copy(out[0], i0), dv(out[4], two(out, in_)) if idx is None else (0.05, 0, out[4], 0))
+
+    def ts(out, in0, s1, op0, s2=None, op1=None, free=False, idx=None):
+        do({"V": a_ts(out, in0, s1, op0, s2, op1, idx)}, [in0] + sca(s1) + sca(s2) + lst(idx), [out], free)
+
+    def tt(out, in0, in1, op, idx=None):
+        i0 = ind(in0, idx)
+        w = (0.05, 0, out[4], 0) if idx else dv(out[4] * (1 if in0[1] in PSUM or in1[1] in PSUM else 2))
+        do({"V": (lambda e: e.tensor_tensor(out[0], i0, in1[0], op), w)}, [in0, in1] + lst(idx), [out])
+
+    def cp(out, in_, idx=None):
+        do({"V": a_cp(out, in_, idx)}, [in_] + lst(idx), [out])
+
+    def fill(out, c):
+        do({"V": (lambda e: e.memset(out[0], c), dv(out[4], two(out)))}, [], [out])
+
+    def scatter(win, idx, in_):
+        do({"V": (lambda e: e.tensor_copy(win[0].indirect(idx[0]), in_[0]), (0.05, 0, 2 * in_[4], 0))}, [in_, idx], [win])
+
+    def scan(out, d0, d1, init, op0, op1):
+        do({"V": (lambda e: e.tensor_tensor_scan(out[0], d0[0], d1[0], init, op0, op1), dv(out[4]))}, [d0, d1], [out])
+
+    def reduce(out, in_, op):
+        do({"V": (lambda e: e.tensor_reduce(out[0], in_[0], AxisListType.X, op), dv(in_[4]))}, [in_], [out])
+
+    def act(out, in_, scale=1.0, bias=0.0, func=AF.Identity, idx=None):
+        do({"S": a_act(out, in_, scale, bias, func, idx)}, [in_] + sca(scale) + sca(bias) + lst(idx), [out])
+
+    def move(out, in_, idx=None):
+        do({"S": a_act(out, in_, idx=idx), "V": a_cp(out, in_, idx)}, [in_] + lst(idx), [out])
+
+    def scale(out, in_, col, free=False):
+        do({"S": a_act(out, in_, col), "V": a_ts(out, in_, col, OP.mult)}, [in_, col], [out], free)
+
+    def mms(out, pairs):
+        n = len(pairs)
+
+        def fn(e):
+            for k in range(n):
+                r = e.matmul(out[0], pairs[k][0][0], pairs[k][1][0], k == 0, k == n - 1)
+            return r
+        do({"P": (fn, (0, 0, 0, n * max(64, out[4])))}, [p for pr in pairs for p in pr], [out])
+
+    def iota(out, pattern, base=0, cm=0):
+        if out[1] == "pi":
+            fn = lambda e: e.iota(out[0], pattern, base, cm)
+        else:
+            fn = lambda e: e.iota(out[0], pattern, base, cm, allow_small_or_imprecise_dtypes=True)
+        return do({"G": (fn, (0.13, 2 * out[4], 0, 0))}, [], [out])
+
+    dma("Y", view("wd", 0, 4), T.ex[:], "dex", 0.1)
+    dma("Y", view("wd", 4, 16), T.zs[:], "dzs", 0.1)
+    c0 = [sum(CWS[:h]) for h in range(NCH)]
+    for h in range(NCH):
+        dma("Y", view("mti", c0[h], c0[h] + CWS[h]), T.mt[:, c0[h]:c0[h] + CWS[h]], "dmt%d" % h, 5.2 * CWS[h] / 4096)
+    dma("S", view("bki"), T.bk[:], "dbk", 0.1)
+    dma("S", view("qci"), T.qc[:], "dqc", 0.1)
+    dma("S", view("qsi"), T.qs[:], "dqs", 0.1)
+
+    dst = T.cores[(rank - 1) % len(T.cores)]
+    rid, pid, _ = topo.addr(dst)
+    emask = topo.mask(core, dst)
+    neng = len(topo.engines(core, dst))
+
+    def send(h):
+        a, b = c0[h], c0[h] + CWS[h]
+        v = view("mti", a, b)
+        i = do({"G": (lambda e: e.remote_dma(T.raw[:, a:b], v[0], T.sem["arr%d" % h], T.sem.sent, pid, rid, emask), (1.0, 0, 0, 0))}, [v], [], tok=())
+        chain("G", i)
+        flight(i, [view("raw", a, b)], 5.2 * CWS[h] / 4096, ("arr%d" % h, neng), 1.0)
+    for h in range(NCH):
+        send(h)
+
+    iota(view("pi", 0, 1), [[0, 1]], 0, 1)
+    iota(view("qg"), [[1, 8], [0, 16]])
+    iota(view("qm"), [[0, 8], [1, 16]], 1)
+    iota(view("c16"), [[16, 16]], 1)
+    iota(view("pg"), [[0, 16], [1, 8]])
+    iota(view("c8"), [[16, 8]])
+    iota(view("c15f"), [[-1, 16]], 15)
+    iota(view("io640"), [[1, 640]])
+    pi = view("pi", 0, 1)
+    ts(view("pi", 4, 5), pi, 15, OP.bitwise_and)
+    ts(view("pi", 5, 6), pi, 4, OP.arith_shift_right)
+    ts(view("pi", 6, 7), pi, 7, OP.bitwise_and)
+    ts(view("pi", 7, 8), pi, 3, OP.arith_shift_right)
+    cp(view("ix", 0, 4), view("pi", 4, 8))
+
+    def ix(k):
+        return view("ix", k, k + 1)
+    A_, G_, PG_, PI_ = ix(0), ix(1), ix(2), ix(3)
+    A1, PI1, A15 = ix(4), ix(5), ix(7)
+    ts(A1, A_, 1.0, OP.add)
+    ts(view("blk"), view("qg"), G_, OP.is_equal)
+    ts(view("eqm"), view("qm"), A1, OP.is_equal)
+    tt(view("i128"), view("eqm"), view("blk"), OP.mult)
+    ts(view("b8f", 0, 8), view("pg", 0, 8), G_, OP.is_equal)
+    ts(view("b8f", 8, 16), view("b8f", 0, 8), -2048.0, OP.mult)
+    cp(view("wdf", 0, 16), view("wd"))
+    ts(view("wdf", 16, 20), view("wdf", 0, 16, 4), 16.0, OP.mult, 1.0, OP.add)
+    tt(view("wdf", 20, 24), view("wdf", 16, 20), view("wdf", 1, 16, 4), OP.add)
+    ts(view("cole"), view("c16"), A_, OP.add)
+    for k in range(4):
+        scale(view("dd", 128 * k, 128 * k + 128), view("i128"), view("wdf", 20 + k, 21 + k))
+    mms(view("pa0"), [(view("blk"), view("dd"))])
+    act(view("wrb"), view("pa0"))
+    for k in range(8):
+        c = 4 * (k % 4) + 2 + k // 4
+        scale(view("dm", 16 * k, 16 * k + 16), view("eqm", 0, 16), view("wdf", c, c + 1))
+    mms(view("pa1", 0, 128), [(view("blk"), view("dm"))])
+    ts(view("msk"), view("pa1", 0, 128), A_, OP.is_equal)
+
+    def sel(kind, s, i, w=128):
+        c = 2048 + 384 * i + 128 * (s - 1) if kind == 0 and s else 2048 * (4 * kind + s) + 128 * i
+        return view("sel", c, c + w)
+
+    def build0(s, w):
+        for i in range(16):
+            ts(sel(0, s, i, w), view("wrb", 128 * s, 128 * s + w), view("cole", i, i + 1), OP.is_equal, free=True)
+
+    def build(kind, s):
+        c = 2048 * (4 * kind + s)
+        m = 16 * (4 * (kind - 1) + s)
+        for k in range(8):
+            scale(view("sel", c + 16 * k, c + 2048, 129), view("msk", m, m + 16), view("b8f", k, k + 1), free=True)
+
+    def jj(i):
+        return view("jj", 128 * i, 128 * i + 128)
+    tt(view("jb"), view("qm"), view("blk"), OP.mult)
+    for i in range(16):
+        ts(jj(i), view("jb"), float(i + 1), OP.is_equal, free=True)
+    for k in (4, 8):
+        fill(view("sel", 2048 * k, 2048 * k + 2048), 0.0)
+    for k in (5, 9, 6, 10, 7, 11):
+        chain("G", iota(view("sel", 2048 * k, 2048 * k + 2048), [[0, 2048]]))
+
+    cp(view("bkl"), view("bki"))
+    cp(view("qcl"), view("qci"))
+    ts(view("qsf"), view("qsi"), 1.0 / 16384, OP.mult)
+    act(view("lrow"), view("io640"), idx=view("qcl"))
+    ts(view("lm"), view("lrow"), A_, OP.is_equal)
+    fill(view("xk", 128, 640), 0.0)
+    fill(view("cnt", 0, 1), 128.0)
+    build0(0, 128)
+    build(1, 0)
+
+    for h in range(NCH):
+        a, b = c0[h], c0[h] + CWS[h]
+        ts(view("wt", a, b), view("raw", a, b), -7.5, OP.add, C27, OP.add)
+        act(view("xw", a, b), view("wt", a, b), scale=0.0625, bias=-C27 / 16)
+    for k in range(8):
+        a = 512 * k
+        bank = view(("pc0", "pc1", "pb0", "pb1")[k % 4])
+        act(bank, view("wt", a, a + 512), bias=-C27)
+        tt(view("ow", a, a + 512), view("raw", a, a + 512), bank, OP.subtract)
+    build(2, 0)
+    build(1, 1)
+    build(2, 1)
+
+    def consts():
+        ts(PI1, PI_, 1.0, OP.add)
+        ts(A15, A_, -1.0, OP.mult, 15.0, OP.add)
+        for t in range(3):
+            ts(ix(8 + t), A_, float(t), OP.not_equal)
+            ts(ix(12 + t), A_, float(t), OP.is_equal)
+        ts(ix(11), A_, 3.0, OP.is_ge)
+        fill(view("neg1"), -1.0)
+        fill(view("z8"), 0.0)
+        fill(view("zb"), 0.0)
+        ts(view("zb", 120, 128), view("pg", 0, 8), G_, OP.is_equal)
+        ts(view("blki"), view("pg"), G_, OP.is_equal)
+        ts(view("blkpp"), view("pg"), PG_, OP.is_equal)
+        ts(view("blkp"), view("qg"), PG_, OP.is_equal)
+        ts(view("tmp"), view("qm"), PI1, OP.is_equal)
+        tt(view("pmx"), view("tmp"), view("blkp"), OP.mult)
+        ts(view("tmp2"), view("qm"), PI1, OP.is_gt, -1.0, OP.add)
+        tt(view("tmb"), view("tmp2"), view("blkp"), OP.mult)
+        ts(view("npm"), view("c8"), PI_, OP.add)
+        ts(view("cnp"), view("npm"), -511.0, OP.add)
+        ts(view("nlneg"), view("c8"), A_, OP.add)
+        ts(view("nlneg"), view("nlneg"), -1.0, OP.mult, 639.0, OP.add)
+        tt(view("c15"), view("eqm", 0, 16), view("c15f"), OP.mult)
+        for t in range(3):
+            scale(view("keep", 128 * t, 128 * t + 128), view("i128"), ix(8 + t))
+        ts(view("nj"), jj(2), -2.0, OP.mult)
+        move(view("num", 0, 128), view("io640", 0, 128))
+        fill(view("rn"), -1.0)
+        fill(view("pzn"), 0.0)
+
+    xw, ow = view("xw"), view("ow")
+    rot = {"g3": 0, "g4": 0}
+
+    def buf(kind):
+        rot[kind] += 1
+        return view("%s%d" % (kind, rot[kind] % 4))
+
+    def lookup(t):
+        if t == 0:
+            ts(view("ki"), view("qsf", 0, 8), 128.0, OP.mult, -EPS, OP.add)
+        else:
+            ts(view("ki"), view("qsf", 8 * t, 8 * t + 8), view("pd0", 8, 9), OP.mult, -EPS, OP.add)
+        cp(view("kl"), view("ki"))
+        if t:
+            scatter(view("xk"), view("pl%d" % (t - 1)), view("xi"))
+        tt(view("qgt"), view("xk"), view("lm", 128 * t, 128 * t + 128), OP.mult, idx=view("kl"))
+        mms(view("pa0", 0, 8), [(jj(i), view("qgt", i, 128, 16)) for i in range(16)])
+        ts(view("ql"), view("pa0", 0, 8), 2048.0, OP.add)
+
+    def pass1(b):
+        lst_ = view("bkl") if b == 0 else view("ql")
+        cp(view("xl%d" % (b % 2)), xw, idx=lst_)
+        ts(view("xk", 0, 128) if b == 0 else view("xi"), xw, -2048.0, OP.add, idx=lst_)
+
+    def pass2(b):
+        for h in (0, 1):
+            ts(view("y%d" % (b % 3), 1024 * h, 1024 * h + 1024), xw, -2048.0, OP.add, idx=view("xl%d" % (b % 2), 64 * h, 64 * h + 64))
+
+    def psel_x(b, out):
+        for h in (0, 1):
+            bank = view("pa%d" % h, 0, 64)
+            mms(bank, [(sel(0, 0, a), view("y%d" % (b % 3), 1024 * h + a, 1024 * h + 1024, 16)) for a in range(16)])
+            ts(view(out, 64 * h, 64 * h + 64), bank, 2048.0, OP.add)
+
+    def psel_z(b, z):
+        bank = view("pe0", 0, 128)
+        mms(bank, [(sel(0, 1 + z, a), view("y%d" % (b % 3), a, 2048, 16)) for a in range(16)])
+        move(view("pz%d" % z, 128 * b, 128 * b + 128), bank)
+
+    def p3(s, src, out):
+        for h in (0, 1):
+            g3 = buf("g3")
+            ts(g3, xw, -2048.0, OP.add, idx=view(src, 64 * h, 64 * h + 64))
+            bank = view("pa%d" % h, 0, 64)
+            mms(bank, [(sel(1, s, e), view(g3[1], e, 1024, 16)) for e in range(16)])
+            ts(view(out, 64 * h, 64 * h + 64), bank, 2048.0, OP.add)
+
+    def p4g(h, src):
+        g4 = buf("g4")
+        move(g4, ow, idx=view(src, 64 * h, 64 * h + 64))
+        return g4
+
+    def p4s(s, h, g4, extra=(), skip=0):
+        bank = view("pb%d" % h, 0, 64)
+        mms(bank, [(sel(2, s, e), view(g4[1], e, 1024, 16)) for e in range(skip, 16)] + list(extra))
+        return bank
+
+    def p4(s, src, evac):
+        for h in (0, 1):
+            evac(h, p4s(s, h, p4g(h, src)))
+
+    def evac_r(b):
+        return lambda h, bank: move(view("rr", 128 * b + 64 * h, 128 * b + 64 * h + 64), bank)
+
+    def evac_aq(h, bank):
+        move(view("aq", 64 * h, 64 * h + 64), bank)
+
+    def differ(h, bank):
+        tt(view("ne", 64 * h, 64 * h + 64), bank, view("aq", 64 * h, 64 * h + 64), OP.not_equal)
+
+    def compare(t):
+        b, L = t + 1, 128 * (t + 1)
+        act(view("r2", 0, L), view("rr", 0, L), scale=32.0, func=AF.Square)
+        for hh in (0, 1):
+            q = view("rr", 128 * b + 64 * hh, 128 * b + 64 * hh + 64)
+            act(view("rq2", 64 * hh, 64 * hh + 64), q, scale=32.0, func=AF.Square)
+            for k in range(8):
+                scale(view("lhb", 512 * hh + k, 512 * hh + 512, 8), q, view("b8f", 8 + k, 9 + k), free=True)
+            for c in range(4 * hh, 4 * hh + 4):
+                bank = view(("pc0", "pc1", "pe0")[c % NB], 0, L)
+                mms(bank, [(view("blki"), view("r2", 0, L)), (view("lhb", 128 * c, 128 * c + 128), view("rr", 0, L))])
+                scan(view("sc", 384 * c, 384 * c + L), bank, view("neg1", 0, L), 8000000.0, OP.min, OP.add)
+        mms(view("pd0", 0, 8), [(view("zb", 120 - 8 * i, 248 - 8 * i), view("rq2", i, 128, 16)) for i in range(16)])
+        act(view("nn"), view("pd0", 0, 8), scale=-1.0)
+
+    def append(t):
+        L, b = 128 * (t + 1), t + 1
+        last = (T.sc[:, L - 1::384], "sc", 0, 3072, 8)
+        tt(view("uu"), last, view("nn"), OP.is_ge)
+        scan(view("inc"), view("uu"), view("z8"), 0.0, OP.add, OP.add)
+        tt(view("vl"), last, view("nn"), OP.subtract)
+        tt(view("ww"), view("uu"), view("cnp"), OP.mult)
+        mms(view("pd0", 8, 9), [(view("i128"), view("cnt", t, t + 1)), (view("blkp"), view("inc", 7, 8))])
+        mms(view("pd0", 0, 8), [(view("blkp"), view("inc")), (view("tmb"), view("uu")), (view("i128"), view("nlneg")), (view("pmx"), view("ww"))])
+        if t < 2:
+            mms(view("pd0", 9, 10), [(view("blkpp"), view("inc", 7, 8))])
+        tt(view("mn"), view("vl"), view("npm"), OP.min)
+        mms(view("pc0", 0, 8), [(view("pmx"), view("mn"))])
+        cp(view("pl%d" % t), view("pd0", 0, 8))
+        if t < 2:
+            lookup(t + 1)
+            cp(view("cnt", t + 1, t + 2), view("pd0", 8, 9))
+            ts(view("cnp"), view("cnp"), view("pd0", 9, 10), OP.add)
+        ts(view("ml"), view("pc0", 0, 8), float(L), OP.add)
+        nb = view("num", 128 * b, 128 * b + 128)
+        move(nb, view("io640"), idx=view("pl%d" % t))
+        move(view("ymt", 128 * t, 128 * t + 128), view("num", 0, 128 * b + 128), idx=view("ml"))
+        ts(view("lm3"), view("pz%d" % t, 0, L + 128), 2048.0, OP.add, idx=view("ml"))
+        if t < 2:
+            q = view("rr", 128 * b, 128 * b + 128)
+            ts(view("inv"), nb, 512.0, OP.is_ge, 16.0, OP.mult)
+            tt(q, q, view("inv"), OP.max)
+        else:
+            ts(view("invn"), view("io640", 0, 512), view("pd0", 8, 9), OP.is_ge)
+            move(view("pzn", 0, 128), view("pz2", 0, 128))
+            move(view("rn", 0, 128), view("rr", 0, 128))
+            for k in range(3):
+                scatter(view("pzn"), view("pl%d" % k), view("pz2", 128 * k + 128, 128 * k + 256))
+                scatter(view("rn"), view("pl%d" % k), view("rr", 128 * k + 128, 128 * k + 256))
+
+    def winner(t):
+        dc, mx, sc = view("sm", 0, 1), view("sm", 1, 2), view("sm", 2, 3)
+        reduce(dc, view("ne"), OP.add)
+        ts(view("dd2"), view("eqm", 0, 16), dc, OP.mult, 16.0, OP.mult)
+        mms(view("pd0", 16, 32), [(view("blk"), view("dd2")), (view("blk"), view("c15"))])
+        ts(sc, dc, 16.0, OP.mult, A15, OP.add)
+        reduce(mx, view("pd0", 16, 32), OP.max)
+        oh = view("oh", t, t + 1)
+        ts(oh, sc, mx, OP.is_equal)
+        ts(view("ws"), view("wdf", 4 * t + 4, 4 * t + 8), oh, OP.mult)
+        mms(view("pd0", 32, 36), [(view("blk"), view("ws"))])
+        ts(view("mk", 2 * t, 2 * t + 2), view("pd0", 34, 36), A_, OP.is_equal)
+        ts(view("ya", 4 * t, 4 * t + 4), view("pd0", 32, 36), ix(12 + t), OP.mult)
+
+    def wpass(t, c0, c1, src):
+        n = (c1 - c0) // 16
+        ts(view("pw", c0, c1), view(src, c0, c1), view("oh", t, t + 1), OP.mult)
+        bank, bank2 = view("pc0", 0, n), view("pc1", 0, n)
+        mms(bank, [(jj(i), view("pw", c0 + i, c1, 16)) for i in range(16)])
+        lw, lw2, gw = view("lw", 0, n), view("lw2", 0, n), view("gw", 0, c1 - c0)
+        ts(lw, bank, 2048.0, OP.add)
+        ts(gw, xw, -2048.0, OP.add, view("mk", 2 * t, 2 * t + 1), OP.mult, idx=lw)
+        mms(bank2, [(jj(i), view("gw", i, c1 - c0, 16)) for i in range(16)])
+        ts(lw2, bank2, 2048.0, OP.add)
+        act(view("gz%d" % t, c0, c1), ow, scale=view("mk", 2 * t + 1, 2 * t + 2), idx=lw2)
+
+    def rupdate(t):
+        L = 128 * (t + 2)
+        bank = view("pc0", 0, L)
+        mms(bank, [(view("keep", 128 * t, 128 * t + 128), view("rr", 0, L)), (jj(t), view("gz%d" % t, 0, L))])
+        move(view("rr", 0, L), bank)
+
+    pass1(0)
+    lookup(0)
+    pass1(1)
+    pass2(0)
+    psel_x(0, "l30")
+    pass2(1)
+    psel_x(1, "l31")
+    p3(0, "l30", "l40")
+    p3(0, "l31", "l41")
+    build0(1, 384)
+    p4(0, "l40", evac_r(0))
+    p4(0, "l41", evac_r(1))
+    consts()
+    psel_z(1, 0)
+    psel_z(0, 0)
+    compare(0)
+    ts(view("l32"), view("pz0", 128, 256), 2048.0, OP.add)
+    p3(1, "l32", "l42")
+    p4(1, "l42", evac_aq)
+    for t in range(3):
+        b = t + 2
+        append(t)
+        p3(1 + t, "lm3", "l43")
+        if t < 2:
+            pass1(b)
+            pass2(b)
+            psel_x(b, "l31")
+        p4(1 + t, "l43", differ)
+        winner(t)
+        if t == 0:
+            for k in (1, 2):
+                for z in (1, 2):
+                    build(k, 1 + z)
+        if t < 2:
+            for z in (0, 1):
+                psel_z(b, z)
+            if t == 0:
+                for bb in (1, 0):
+                    psel_z(bb, 1)
+            p3(0, "l31", "l41")
+        c1 = min(512, 128 * (t + 3))
+        wpass(t, 0, c1, "pzn" if t == 2 else "pz%d" % t)
+        if t == 1:
+            wpass(0, 384, 512, "pz0")
+        if t == 2:
+            break
+        gs = [p4g(h, "l41") for h in (0, 1)]
+        rupdate(t)
+        for h in (0, 1):
+            c = 128 * b + 64 * h
+            evac_r(b)(h, p4s(0, h, gs[h], [(jj(k), view("gz%d" % k, c, c + 64)) for k in range(t + 1)], t + 1))
+        if t == 0:
+            for bb in (1, 0):
+                psel_z(bb, 2)
+        psel_z(b, 2)
+        compare(t + 1)
+        ts(view("l32"), view("pz%d" % (t + 1), 128 * b, 128 * b + 128), 2048.0, OP.add)
+        p3(2 + t, "l32", "l42")
+        p4(2 + t, "l42", evac_aq)
+
+    ends = []
+
+    def out(dst_ap, src_ap, v, sem):
+        do({"Y": (lambda e: e.dma_start(dst_ap, src_ap).then_inc(T.sem[sem], 16), (0.1, 0, 0, 0))}, [v], [], lat=2.0, tok=())
+        ends.append(sem)
+    out(T.ym[:], T.ymt[::16, :], view("ymt"), "dym")
+    yet = view("ya", 12, 16)
+    ts(yet, view("wdf", 0, 4), ix(11), OP.mult)
+    for t in range(3):
+        tt(yet, yet, view("ya", 4 * t, 4 * t + 4), OP.add)
+    out(T.ye[:], T.ya[:, 12:16], yet, "dye")
+    mms(view("pc0"), [(view("keep", 256, 384), view("rn", 0, 512)), (view("nj"), view("invn")), (jj(2), view("gz2"))])
+    ts(view("yrt"), view("pc0"), -1.0, OP.max)
+    out(T.yr[:], T.yrt[:], view("yrt"), "dyr")
+
+    if "p" not in PLAN:
+        PLAN["p"] = plan(ops)
+        PLAN["ops"] = ops
+    pos = {q: 0 for q in queue}
+    seen = {q: {} for q in queue}
+    for i, q in PLAN["p"][2]:
+        o = ops[i]
+        o["run"] = q
+        if q == "D":
+            continue
+        want = {}
+        for d in o["deps"] | set(d for d in o["soft"] if ops[d]["run"] != q):
+            if ops[d]["tok"]:
+                s, n = ops[d]["tok"]
+                want[s] = max(want.get(s, 0), n)
+        for s in sorted(want):
+            if seen[q].get(s, 0) < want[s]:
+                queue[q].wait_ge(T.sem[s], want[s])
+                seen[q][s] = want[s]
+        r = o["alt"][q][0](queue[q])
+        if o["tok"] is None:
+            pos[q] += 1
+            r.then_inc(T.sem[CSEM[q]], 1)
+            o["tok"] = (CSEM[q], pos[q])
+    for s in ends:
+        g.sync.wait_ge(T.sem[s], 16)
+    g.wait_ge(T.sem.sent, NCH * neng)
+    for q in sorted(CSEM):
+        g.wait_ge(T.sem[CSEM[q]], pos[q])

@@ -7,33 +7,34 @@ CWS = [1024, 1024, 1024, 512, 512]
 NCH = len(CWS)
 C27 = 201326592.0
 EPS = 0.499969482421875
-COSTS = [(0.00100, 1.5, 0.00042, 0.10), (0.00090, 1.2, 0.00042, 0.05), (0.00105, 1.9, 0.0006, 0.15)]
-TRIES = 1000
-SEED = 3
-NB = 3
+COSTS = [(0.00095, 1.45, 0.00052, 0.10, 1.0, 2.0), (0.00090, 1.1, 0.00050, 0.10, 1.0, 4.0), (0.0012, 1.9, 0.0006, 0.15, 1.3, 2.0),
+         (0.00095, 1.4, 0.00075, 0.10, 1.0, 2.0), (0.00095, 1.45, 0.0005, 0.12, 2.0, 8.0), (0.00095, 1.4, 0.0005, 0.25, 1.2, 2.0)]
+STARTS, SHORT, LONG = 4, 350, 900
+HOW = {"B": "SS", "q0": "VV", "z0": "SS", "z1": "VV", "z2": "VV", "m0": "VV", "m1": "VV", "m2": "VV", "q1": "VV", "q2": "VV"}
+PARTS = 4
 
 F, B, H, I, U = "float32", "bfloat16", "float16", "int32", "uint16"
 SCRATCH = {}
 for _n, _w, _d in [
         ("mti", 4096, I), ("raw", 4096, I), ("wt", 4096, F), ("xw", 4096, F), ("ow", 4096, B),
         ("wd", 16, I), ("bki", 8, I), ("qsi", 24, I), ("qci", 24, I), ("pi", 8, I), ("ix", 24, F),
-        ("qg", 128, F), ("qm", 128, F), ("pg", 128, F), ("c16", 16, F), ("io640", 640, F), ("c8", 8, F),
-        ("blk", 128, B), ("eqm", 128, B), ("i128", 128, B), ("jb", 128, B), ("jj", 2048, B), ("nj", 128, B),
-        ("blkp", 128, B), ("tmp", 128, B), ("tmp2", 128, B), ("tmb", 128, B), ("pmx", 128, B), ("blkpp", 128, B), ("blki", 128, B),
+        ("qg", 128, F), ("qm", 128, F), ("pg", 128, F), ("c16", 32, F), ("io640", 640, F), ("c8", 8, F),
+        ("blk", 128, B), ("eqm", 128, B), ("i128", 128, B), ("jb", 16, B), ("jj", 2048, B), ("nj", 128, B),
+        ("blkp", 128, B), ("tmp", 256, B), ("tmb", 128, B), ("pmx", 128, B), ("blkpp", 128, B), ("blki", 128, B),
         ("zb", 248, B), ("b8f", 16, F), ("keep", 384, B), ("cole", 16, F), ("nlneg", 8, H), ("npm", 8, F), ("cnp", 8, F),
-        ("neg1", 384, F), ("z8", 8, F), ("c15", 16, B), ("c15f", 16, F),
+        ("neg1", 384, F), ("z8", 8, F), ("c15", 16, B),
         ("wdf", 24, F), ("dd", 512, B), ("wrb", 512, B), ("dm", 128, B), ("msk", 128, B),
-        ("sel", 12 * 2048, B), ("qcl", 24, U), ("lrow", 384, F), ("lm", 384, B), ("qsf", 24, F), ("bkl", 8, U),
+        ("sel", 9 * 2048, B), ("st", 512, B), ("sf", 4096, F), ("qcl", 24, U), ("lrow", 384, F), ("lm", 384, B), ("qsf", 24, F), ("bkl", 8, U),
         ("ki", 8, I), ("kl", 8, U), ("qgt", 128, H), ("ql", 8, U), ("xi", 128, F), ("xl0", 128, U), ("xl1", 128, U), ("xk", 640, F),
-        ("y0", 2048, H), ("y1", 2048, H), ("y2", 2048, H),
+        ("y0", 2048, H), ("y1", 2048, H), ("y2", 2048, H), ("gf", 2048, F),
         ("g30", 1024, H), ("g31", 1024, H), ("g32", 1024, H), ("g33", 1024, H),
-        ("g40", 1024, B), ("g41", 1024, B), ("g42", 1024, B), ("g43", 1024, B),
+        ("g40", 1024, B), ("g41", 1024, B), ("g42", 1024, B), ("g43", 1024, B), ("gt", 2048, B),
         ("l30", 128, U), ("l31", 128, U), ("l32", 128, U), ("lm3", 128, U),
         ("l40", 128, U), ("l41", 128, U), ("l42", 128, U), ("l43", 128, U),
         ("pz0", 512, F), ("pz1", 512, F), ("pz2", 512, F), ("pzn", 640, F), ("rr", 512, B), ("rn", 640, B), ("invn", 512, B),
         ("r2", 384, B), ("rq2", 128, B), ("lhb", 1024, B),
         ("sc", 3072, F), ("nn", 8, F), ("vl", 8, F), ("uu", 8, H), ("inc", 8, H), ("ww", 8, H), ("mn", 8, H), ("ml", 8, U), ("cnt", 4, H),
-        ("pl0", 8, U), ("pl1", 8, U), ("pl2", 8, U), ("num", 512, F), ("ymt", 384, F), ("inv", 128, B),
+        ("pl", 24, U), ("num", 512, F), ("ymt", 384, F), ("inv", 128, B),
         ("aq", 128, B), ("ne", 128, B), ("sm", 8, F), ("dd2", 16, B), ("oh", 4, F), ("ws", 4, B),
         ("mk", 8, F), ("ya", 16, F), ("pw", 512, H), ("lw", 32, U), ("gw", 512, H), ("lw2", 32, U),
         ("gz0", 512, B), ("gz1", 512, B), ("gz2", 512, B), ("yrt", 512, F)]:
@@ -47,7 +48,8 @@ PLAN = {}
 
 
 def cost(w, c):
-    return w[0] + c[0] * (w[1] + c[1] * w[2]) + c[2] * w[3]
+    t = w[0] + c[0] * (w[1] + c[1] * w[2]) + c[2] * w[3]
+    return t + c[4] * w[4] + c[5] * w[5] if len(w) > 4 else t
 
 
 def evaluate(ops, order, c):
@@ -62,28 +64,33 @@ def evaluate(ops, order, c):
                 s = max(s, fin[d] + c[3])
         e = s + cost(o["alt"][q][1], c)
         free[q] = e
-        fin[i] = e + o["lat"]
+        fin[i] = e + o["lat"] * c[4]
         end = max(end, fin[i])
     return end
 
 
-def place(ops, pre, succ, pr, al, durs, hop):
+def place(ops, pre, succ, pr, al, durs, hop, back=False):
     n = len(ops)
     pr = list(pr)
-    for i in range(n - 1, -1, -1):
+    for i in (range(n) if back else range(n - 1, -1, -1)):
         for s in succ[i]:
             if pr[i] <= pr[s]:
                 pr[i] = pr[s] + 1e-6
-    line, fin, got = {}, [0.0] * n, []
+    line, fin, beg = {}, [0.0] * n, [0.0] * n
     for i in sorted(range(n), key=lambda x: -pr[x]):
         o = ops[i]
         best = None
-        for x, q in enumerate(o["alt"]):
-            if len(o["alt"]) > 1 and ((al[i] > 0.75 and x == 0) or (0.5 < al[i] <= 0.75 and x == 1)):
+        for x, q in enumerate([o["run"]] if back else o["alt"]):
+            if not back and len(o["alt"]) > 1 and ((al[i] > 0.75 and x == 0) or (0.5 < al[i] <= 0.75 and x == 1)):
                 continue
-            t = 0.0
+            t = o["lat"] if back else 0.0
             for d in pre[i]:
-                t = max(t, fin[d] + (0.0 if ops[d]["run"] == q and d in o["soft"] else ops[d]["lat"] + hop))
+                if back:
+                    y = fin[d] + (0.0 if ops[d]["run"] == q and i in ops[d]["soft"] else o["lat"] + hop)
+                else:
+                    y = fin[d] + (0.0 if ops[d]["run"] == q and d in o["soft"] else ops[d]["lat"] + hop)
+                if y > t:
+                    t = y
             s, e = line.setdefault(q, ([], []))
             w = durs[i][q]
             k = len(s)
@@ -97,16 +104,17 @@ def place(ops, pre, succ, pr, al, durs, hop):
         f, t, q, k = best
         line[q][0].insert(k, t)
         line[q][1].insert(k, f)
-        o["run"] = q
+        if not back:
+            o["run"] = q
         fin[i] = f
-        got.append((t, len(got), i, q))
-    got.sort()
-    return [(i, q) for _, _, i, q in got]
+        beg[i] = t
+    return beg, fin
 
 
 def plan(ops):
     n = len(ops)
     c = COSTS[0]
+    hop = c[3]
     durs = [{q: cost(o["alt"][q][1], c) for q in o["alt"]} for o in ops]
     pre = [sorted(o["deps"] | o["soft"]) for o in ops]
     succ = [[] for _ in range(n)]
@@ -115,23 +123,34 @@ def plan(ops):
             succ[d].append(i)
     prio = [0.0] * n
     for i in range(n - 1, -1, -1):
-        prio[i] = min(durs[i].values()) + ops[i]["lat"] + max([prio[s] + c[3] for s in succ[i]] + [0.0])
-    rng = np.random.RandomState(SEED)
-    best, bp, bal = None, prio, [0.6] * n
-    for k in range(TRIES):
-        pr, al = bp, bal
-        if k:
+        prio[i] = min(durs[i].values()) + ops[i]["lat"] + max([prio[s] + hop for s in succ[i]] + [0.0])
+    first, top, cur = None, None, None
+    for k in range(STARTS * SHORT + LONG):
+        if k < STARTS * SHORT and k % SHORT == 0:
+            rng, cur = np.random.RandomState(4 + k // SHORT), None
+        elif k == STARTS * SHORT:
+            cur = top
+        if cur is None:
+            pr, al = prio, [0.6] * n
+        else:
             amp = [0.5, 2.0, 6.0, 15.0][k % 4]
             frac = [0.003, 0.01, 0.03, 0.1][(k // 4) % 4]
             x, y, z = rng.rand(n).tolist(), rng.rand(n).tolist(), rng.rand(n).tolist()
-            pr = [bp[i] + (amp * (x[i] - 0.5) if y[i] < frac else 0.0) for i in range(n)]
-            al = [(0.45 + 0.4 * z[i] if y[i] < frac else bal[i]) for i in range(n)]
-        order = place(ops, pre, succ, pr, al, durs, c[3])
+            pr = [cur[2][i] + (amp * (x[i] - 0.5) if y[i] < frac else 0.0) for i in range(n)]
+            al = [(0.45 + 0.4 * z[i] if y[i] < frac else cur[3][i]) for i in range(n)]
+        beg, fin = place(ops, pre, succ, pr, al, durs, hop)
+        b2, f2 = place(ops, succ, pre, fin, al, durs, hop, True)
+        beg, fin = place(ops, pre, succ, f2, al, durs, hop)
+        order = [(i, ops[i]["run"]) for i in sorted(range(n), key=lambda x: (beg[x], x))]
         end = [evaluate(ops, order, x) for x in COSTS]
-        score = sum(e / (1.0 + j) for j, e in enumerate(end))
-        if best is None or score < best[0]:
-            best, bp, bal = (score, end, order), pr, al
-    return best
+        if first is None:
+            first = end
+        score = sum(e / f for e, f in zip(end, first)) + end[0] / first[0]
+        if cur is None or score < cur[0]:
+            cur = (score, end, f2, al, order)
+        if top is None or score < top[0]:
+            top = cur
+    return (top[0], top[1], top[4])
 
 
 def rank_program(g, core, T, topo):
@@ -191,7 +210,7 @@ def rank_program(g, core, T, topo):
         chains[q] = i
 
     def flight(i, out, us, tok, lat):
-        j = do({"D": (None, (us, 0, 0, 0))}, [], out, tok=tok, lat=lat, dep=[i])
+        j = do({"D": (None, (0, 0, 0, 0, us, 0))}, [], out, tok=tok, lat=lat, dep=[i])
         chain("D", j)
 
     def dma(q, out, in_ap, sem, us):
@@ -265,14 +284,16 @@ def rank_program(g, core, T, topo):
     def scale(out, in_, col, free=False):
         do({"S": a_act(out, in_, col), "V": a_ts(out, in_, col, OP.mult)}, [in_, col], [out], free)
 
-    def mms(out, pairs):
+    def mms(out, pairs, f=1, parts=1):
         n = len(pairs)
+        for m in range(parts):
+            lo, hi = n * m // parts, n * (m + 1) // parts
 
-        def fn(e):
-            for k in range(n):
-                r = e.matmul(out[0], pairs[k][0][0], pairs[k][1][0], k == 0, k == n - 1)
-            return r
-        do({"P": (fn, (0, 0, 0, n * max(64, out[4])))}, [p for pr in pairs for p in pr], [out])
+            def fn(e, lo=lo, hi=hi):
+                for k in range(lo, hi):
+                    r = e.matmul(out[0], pairs[k][0][0], pairs[k][1][0], k == 0, k == n - 1)
+                return r
+            do({"P": (fn, (0, 0, 0, f * (hi - lo) * max(64, out[4])))}, [p for pr in pairs[lo:hi] for p in pr], [out])
 
     def iota(out, pattern, base=0, cm=0):
         if out[1] == "pi":
@@ -298,7 +319,8 @@ def rank_program(g, core, T, topo):
     def send(h):
         a, b = c0[h], c0[h] + CWS[h]
         v = view("mti", a, b)
-        i = do({"G": (lambda e: e.remote_dma(T.raw[:, a:b], v[0], T.sem["arr%d" % h], T.sem.sent, pid, rid, emask), (1.0, 0, 0, 0))}, [v], [], tok=())
+        i = do({"G": (lambda e: e.remote_dma(T.raw[:, a:b], v[0], T.sem["arr%d" % h], T.sem.sent, pid, rid, emask),
+                      (0, 0, 0, 0, 1.0, 0 if h else 1))}, [v], [], tok=())
         chain("G", i)
         flight(i, [view("raw", a, b)], 5.2 * CWS[h] / 4096, ("arr%d" % h, neng), 1.0)
     for h in range(NCH):
@@ -307,10 +329,10 @@ def rank_program(g, core, T, topo):
     iota(view("pi", 0, 1), [[0, 1]], 0, 1)
     iota(view("qg"), [[1, 8], [0, 16]])
     iota(view("qm"), [[0, 8], [1, 16]], 1)
-    iota(view("c16"), [[16, 16]], 1)
+    iota(view("c16", 0, 16), [[16, 16]], 1)
     iota(view("pg"), [[0, 16], [1, 8]])
     iota(view("c8"), [[16, 8]])
-    iota(view("c15f"), [[-1, 16]], 15)
+    iota(view("c16", 16, 32), [[-1, 16]], 15)
     iota(view("io640"), [[1, 640]])
     pi = view("pi", 0, 1)
     ts(view("pi", 4, 5), pi, 15, OP.bitwise_and)
@@ -332,7 +354,7 @@ def rank_program(g, core, T, topo):
     cp(view("wdf", 0, 16), view("wd"))
     ts(view("wdf", 16, 20), view("wdf", 0, 16, 4), 16.0, OP.mult, 1.0, OP.add)
     tt(view("wdf", 20, 24), view("wdf", 16, 20), view("wdf", 1, 16, 4), OP.add)
-    ts(view("cole"), view("c16"), A_, OP.add)
+    ts(view("cole"), view("c16", 0, 16), A_, OP.add)
     for k in range(4):
         scale(view("dd", 128 * k, 128 * k + 128), view("i128"), view("wdf", 20 + k, 21 + k))
     mms(view("pa0"), [(view("blk"), view("dd"))])
@@ -351,21 +373,40 @@ def rank_program(g, core, T, topo):
         for i in range(16):
             ts(sel(0, s, i, w), view("wrb", 128 * s, 128 * s + w), view("cole", i, i + 1), OP.is_equal, free=True)
 
-    def build(kind, s):
-        c = 2048 * (4 * kind + s)
-        m = 16 * (4 * (kind - 1) + s)
+    def selF(s, i, w=128):
+        return view("sf", 2048 * s + 128 * i, 2048 * s + 128 * i + w)
+
+    def spread(v, m, st):
         for k in range(8):
-            scale(view("sel", c + 16 * k, c + 2048, 129), view("msk", m, m + 16), view("b8f", k, k + 1), free=True)
+            scale(view(v[1], v[2] + (16 * k if st == 129 else k), v[3], st), view("msk", m, m + 16), view("b8f", k, k + 1), free=True)
+
+    def buildF(s):
+        spread(selF(s, 0, 2048), 16 * s, 129)
+
+    def build(kind, s):
+        spread(sel(kind, s, 0, 2048), 16 * (4 * (kind - 1) + s), 129)
+
+    def buildT(s):
+        spread(view("st", 128 * s, 128 * s + 128), 16 * (4 + s), 8)
 
     def jj(i):
         return view("jj", 128 * i, 128 * i + 128)
-    tt(view("jb"), view("qm"), view("blk"), OP.mult)
-    for i in range(16):
-        ts(jj(i), view("jb"), float(i + 1), OP.is_equal, free=True)
-    for k in (4, 8):
-        fill(view("sel", 2048 * k, 2048 * k + 2048), 0.0)
-    for k in (5, 9, 6, 10, 7, 11):
-        chain("G", iota(view("sel", 2048 * k, 2048 * k + 2048), [[0, 2048]]))
+
+    def const(v, c=0):
+        chain("G", iota(v, [[0, v[4]]], c))
+
+    def zero(k):
+        const(view("sel", 2048 * k, 2048 * k + 2048))
+    fill(view("jj"), 0.0)
+    const(selF(0, 0, 2048))
+    zero(4)
+    zero(8)
+    const(selF(1, 0, 2048))
+    const(view("neg1"), -1)
+    zero(5)
+    fill(view("jb"), 1.0)
+    for k in range(8):
+        scale(view("jj", 16 * k, 2048, 129), view("jb"), view("b8f", k, k + 1), free=True)
 
     cp(view("bkl"), view("bki"))
     cp(view("qcl"), view("qci"))
@@ -386,9 +427,14 @@ def rank_program(g, core, T, topo):
         bank = view(("pc0", "pc1", "pb0", "pb1")[k % 4])
         act(bank, view("wt", a, a + 512), bias=-C27)
         tt(view("ow", a, a + 512), view("raw", a, a + 512), bank, OP.subtract)
+    zero(6)
+    zero(7)
+    const(view("rn"), -1)
+    const(view("pzn"))
+    buildF(0)
     build(2, 0)
     build(1, 1)
-    build(2, 1)
+    buildT(1)
 
     def consts():
         ts(PI1, PI_, 1.0, OP.add)
@@ -397,28 +443,25 @@ def rank_program(g, core, T, topo):
             ts(ix(8 + t), A_, float(t), OP.not_equal)
             ts(ix(12 + t), A_, float(t), OP.is_equal)
         ts(ix(11), A_, 3.0, OP.is_ge)
-        fill(view("neg1"), -1.0)
         fill(view("z8"), 0.0)
         fill(view("zb"), 0.0)
         ts(view("zb", 120, 128), view("pg", 0, 8), G_, OP.is_equal)
         ts(view("blki"), view("pg"), G_, OP.is_equal)
         ts(view("blkpp"), view("pg"), PG_, OP.is_equal)
         ts(view("blkp"), view("qg"), PG_, OP.is_equal)
-        ts(view("tmp"), view("qm"), PI1, OP.is_equal)
-        tt(view("pmx"), view("tmp"), view("blkp"), OP.mult)
-        ts(view("tmp2"), view("qm"), PI1, OP.is_gt, -1.0, OP.add)
-        tt(view("tmb"), view("tmp2"), view("blkp"), OP.mult)
+        ts(view("tmp", 0, 128), view("qm"), PI1, OP.is_equal)
+        tt(view("pmx"), view("tmp", 0, 128), view("blkp"), OP.mult)
+        ts(view("tmp", 128, 256), view("qm"), PI1, OP.is_gt, -1.0, OP.add)
+        tt(view("tmb"), view("tmp", 128, 256), view("blkp"), OP.mult)
         ts(view("npm"), view("c8"), PI_, OP.add)
         ts(view("cnp"), view("npm"), -511.0, OP.add)
         ts(view("nlneg"), view("c8"), A_, OP.add)
         ts(view("nlneg"), view("nlneg"), -1.0, OP.mult, 639.0, OP.add)
-        tt(view("c15"), view("eqm", 0, 16), view("c15f"), OP.mult)
+        tt(view("c15"), view("eqm", 0, 16), view("c16", 16, 32), OP.mult)
         for t in range(3):
             scale(view("keep", 128 * t, 128 * t + 128), view("i128"), ix(8 + t))
         ts(view("nj"), jj(2), -2.0, OP.mult)
         move(view("num", 0, 128), view("io640", 0, 128))
-        fill(view("rn"), -1.0)
-        fill(view("pzn"), 0.0)
 
     xw, ow = view("xw"), view("ow")
     rot = {"g3": 0, "g4": 0}
@@ -427,6 +470,9 @@ def rank_program(g, core, T, topo):
         rot[kind] += 1
         return view("%s%d" % (kind, rot[kind] % 4))
 
+    def pl(t):
+        return view("pl", 8 * t, 8 * t + 8)
+
     def lookup(t):
         if t == 0:
             ts(view("ki"), view("qsf", 0, 8), 128.0, OP.mult, -EPS, OP.add)
@@ -434,7 +480,7 @@ def rank_program(g, core, T, topo):
             ts(view("ki"), view("qsf", 8 * t, 8 * t + 8), view("pd0", 8, 9), OP.mult, -EPS, OP.add)
         cp(view("kl"), view("ki"))
         if t:
-            scatter(view("xk"), view("pl%d" % (t - 1)), view("xi"))
+            scatter(view("xk"), pl(t - 1), view("xi"))
         tt(view("qgt"), view("xk"), view("lm", 128 * t, 128 * t + 128), OP.mult, idx=view("kl"))
         mms(view("pa0", 0, 8), [(jj(i), view("qgt", i, 128, 16)) for i in range(16)])
         ts(view("ql"), view("pa0", 0, 8), 2048.0, OP.add)
@@ -456,39 +502,51 @@ def rank_program(g, core, T, topo):
 
     def psel_z(b, z):
         bank = view("pe0", 0, 128)
-        mms(bank, [(sel(0, 1 + z, a), view("y%d" % (b % 3), a, 2048, 16)) for a in range(16)])
+        mms(bank, [(sel(0, 1 + z, a), view("y%d" % (b % 3), a, 2048, 16)) for a in range(16)], 1, PARTS)
         move(view("pz%d" % z, 128 * b, 128 * b + 128), bank)
 
-    def p3(s, src, out):
+    def p3(s, src, out, who):
+        how = HOW[who]
         for h in (0, 1):
-            g3 = buf("g3")
-            ts(g3, xw, -2048.0, OP.add, idx=view(src, 64 * h, 64 * h + 64))
+            idx = view(src, 64 * h, 64 * h + 64)
             bank = view("pa%d" % h, 0, 64)
-            mms(bank, [(sel(1, s, e), view(g3[1], e, 1024, 16)) for e in range(16)])
-            ts(view(out, 64 * h, 64 * h + 64), bank, 2048.0, OP.add)
+            res = view(out, 64 * h, 64 * h + 64)
+            if how[h] == "V":
+                g3 = buf("g3")
+                ts(g3, xw, -2048.0, OP.add, idx=idx)
+                mms(bank, [(sel(1, s, e), view(g3[1], e, 1024, 16)) for e in range(16)])
+                ts(res, bank, 2048.0, OP.add)
+            else:
+                if how == "SS":
+                    bank = view("pe0", 64 * h, 64 * h + 64)
+                act(view("gf", 1024 * h, 1024 * h + 1024), xw, idx=idx)
+                mms(bank, [(selF(s, e), view("gf", 1024 * h + e, 1024 * h + 1024, 16)) for e in range(16)], 4, PARTS)
+                cp(res, bank)
 
     def p4g(h, src):
         g4 = buf("g4")
         move(g4, ow, idx=view(src, 64 * h, 64 * h + 64))
         return g4
 
-    def p4s(s, h, g4, extra=(), skip=0):
+    def p4s(h, g4, extra=(), skip=0):
         bank = view("pb%d" % h, 0, 64)
-        mms(bank, [(sel(2, s, e), view(g4[1], e, 1024, 16)) for e in range(skip, 16)] + list(extra))
+        mms(bank, [(sel(2, 0, e), view(g4[1], e, 1024, 16)) for e in range(skip, 16)] + list(extra))
         return bank
 
-    def p4(s, src, evac):
+    def p4z(s, src):
         for h in (0, 1):
-            evac(h, p4s(s, h, p4g(h, src)))
+            move(view("gt", 1024 * h, 1024 * h + 1024), ow, idx=view(src, 64 * h, 64 * h + 64))
+        bank, m = view("pb%d" % (s % 2), 0, 128), 128 * s
 
-    def evac_r(b):
-        return lambda h, bank: move(view("rr", 128 * b + 64 * h, 128 * b + 64 * h + 64), bank)
+        def fn(e):
+            for k in range(16):
+                r = e.matmul(T[bank[1]][:, k:128:16], T.gt[:, k:2048:16], T.st[:, m + 8 * k:m + 8 * k + 8], True, True)
+            return r
+        do({"P": (fn, (0, 0, 0, 16 * 64))}, [view("gt"), view("st", m, m + 128)], [bank])
+        return bank
 
-    def evac_aq(h, bank):
-        move(view("aq", 64 * h, 64 * h + 64), bank)
-
-    def differ(h, bank):
-        tt(view("ne", 64 * h, 64 * h + 64), bank, view("aq", 64 * h, 64 * h + 64), OP.not_equal)
+    def evac_r(b, h, bank):
+        move(view("rr", 128 * b + 64 * h, 128 * b + 64 * h + 64), bank)
 
     def compare(t):
         b, L = t + 1, 128 * (t + 1)
@@ -499,7 +557,7 @@ def rank_program(g, core, T, topo):
             for k in range(8):
                 scale(view("lhb", 512 * hh + k, 512 * hh + 512, 8), q, view("b8f", 8 + k, 9 + k), free=True)
             for c in range(4 * hh, 4 * hh + 4):
-                bank = view(("pc0", "pc1", "pe0")[c % NB], 0, L)
+                bank = view("pc%d" % (c % 2), 0, L)
                 mms(bank, [(view("blki"), view("r2", 0, L)), (view("lhb", 128 * c, 128 * c + 128), view("rr", 0, L))])
                 scan(view("sc", 384 * c, 384 * c + L), bank, view("neg1", 0, L), 8000000.0, OP.min, OP.add)
         mms(view("pd0", 0, 8), [(view("zb", 120 - 8 * i, 248 - 8 * i), view("rq2", i, 128, 16)) for i in range(16)])
@@ -518,14 +576,14 @@ def rank_program(g, core, T, topo):
             mms(view("pd0", 9, 10), [(view("blkpp"), view("inc", 7, 8))])
         tt(view("mn"), view("vl"), view("npm"), OP.min)
         mms(view("pc0", 0, 8), [(view("pmx"), view("mn"))])
-        cp(view("pl%d" % t), view("pd0", 0, 8))
+        cp(pl(t), view("pd0", 0, 8))
         if t < 2:
             lookup(t + 1)
             cp(view("cnt", t + 1, t + 2), view("pd0", 8, 9))
             ts(view("cnp"), view("cnp"), view("pd0", 9, 10), OP.add)
         ts(view("ml"), view("pc0", 0, 8), float(L), OP.add)
         nb = view("num", 128 * b, 128 * b + 128)
-        move(nb, view("io640"), idx=view("pl%d" % t))
+        move(nb, view("io640"), idx=pl(t))
         move(view("ymt", 128 * t, 128 * t + 128), view("num", 0, 128 * b + 128), idx=view("ml"))
         ts(view("lm3"), view("pz%d" % t, 0, L + 128), 2048.0, OP.add, idx=view("ml"))
         if t < 2:
@@ -537,12 +595,12 @@ def rank_program(g, core, T, topo):
             move(view("pzn", 0, 128), view("pz2", 0, 128))
             move(view("rn", 0, 128), view("rr", 0, 128))
             for k in range(3):
-                scatter(view("pzn"), view("pl%d" % k), view("pz2", 128 * k + 128, 128 * k + 256))
-                scatter(view("rn"), view("pl%d" % k), view("rr", 128 * k + 128, 128 * k + 256))
+                scatter(view("pzn"), pl(k), view("pz2", 128 * k + 128, 128 * k + 256))
+                scatter(view("rn"), pl(k), view("rr", 128 * k + 128, 128 * k + 256))
 
     def winner(t):
-        dc, mx, sc = view("sm", 0, 1), view("sm", 1, 2), view("sm", 2, 3)
-        reduce(dc, view("ne"), OP.add)
+        dc, mx, sc = view("pd0", 48, 49), view("sm", 1, 2), view("sm", 2, 3)
+        mms(dc, [(view("ne"), view("jb", 0, 1))])
         ts(view("dd2"), view("eqm", 0, 16), dc, OP.mult, 16.0, OP.mult)
         mms(view("pd0", 16, 32), [(view("blk"), view("dd2")), (view("blk"), view("c15"))])
         ts(sc, dc, 16.0, OP.mult, A15, OP.add)
@@ -579,39 +637,41 @@ def rank_program(g, core, T, topo):
     psel_x(0, "l30")
     pass2(1)
     psel_x(1, "l31")
-    p3(0, "l30", "l40")
-    p3(0, "l31", "l41")
+    p3(0, "l30", "l40", "B")
+    p3(0, "l31", "l41", "q0")
     build0(1, 384)
-    p4(0, "l40", evac_r(0))
-    p4(0, "l41", evac_r(1))
+    buildF(1)
+    for b in (0, 1):
+        for h in (0, 1):
+            evac_r(b, h, p4s(h, p4g(h, "l4%d" % b)))
     consts()
     psel_z(1, 0)
     psel_z(0, 0)
     compare(0)
     ts(view("l32"), view("pz0", 128, 256), 2048.0, OP.add)
-    p3(1, "l32", "l42")
-    p4(1, "l42", evac_aq)
+    p3(1, "l32", "l42", "z0")
+    move(view("aq"), p4z(1, "l42"))
     for t in range(3):
         b = t + 2
         append(t)
-        p3(1 + t, "lm3", "l43")
+        p3(1 + t, "lm3", "l43", "m%d" % t)
         if t < 2:
             pass1(b)
             pass2(b)
             psel_x(b, "l31")
-        p4(1 + t, "l43", differ)
+        tt(view("ne"), p4z(1 + t, "l43"), view("aq"), OP.not_equal)
         winner(t)
         if t == 0:
-            for k in (1, 2):
-                for z in (1, 2):
-                    build(k, 1 + z)
+            for z in (1, 2):
+                build(1, 1 + z)
+                buildT(1 + z)
         if t < 2:
             for z in (0, 1):
                 psel_z(b, z)
             if t == 0:
                 for bb in (1, 0):
                     psel_z(bb, 1)
-            p3(0, "l31", "l41")
+            p3(0, "l31", "l41", "q%d" % (t + 1))
         c1 = min(512, 128 * (t + 3))
         wpass(t, 0, c1, "pzn" if t == 2 else "pz%d" % t)
         if t == 1:
@@ -622,15 +682,15 @@ def rank_program(g, core, T, topo):
         rupdate(t)
         for h in (0, 1):
             c = 128 * b + 64 * h
-            evac_r(b)(h, p4s(0, h, gs[h], [(jj(k), view("gz%d" % k, c, c + 64)) for k in range(t + 1)], t + 1))
+            evac_r(b, h, p4s(h, gs[h], [(jj(k), view("gz%d" % k, c, c + 64)) for k in range(t + 1)], t + 1))
         if t == 0:
             for bb in (1, 0):
                 psel_z(bb, 2)
         psel_z(b, 2)
         compare(t + 1)
         ts(view("l32"), view("pz%d" % (t + 1), 128 * b, 128 * b + 128), 2048.0, OP.add)
-        p3(2 + t, "l32", "l42")
-        p4(2 + t, "l42", evac_aq)
+        p3(2 + t, "l32", "l42", "z%d" % (t + 1))
+        move(view("aq"), p4z(2 + t, "l42"))
 
     ends = []
 

@@ -9,9 +9,10 @@ C27 = 201326592.0
 EPS = 0.499969482421875
 COSTS = [(0.00095, 1.45, 0.00052, 0.10, 1.0, 2.0), (0.00090, 1.1, 0.00050, 0.10, 1.0, 4.0), (0.0012, 1.9, 0.0006, 0.15, 1.3, 2.0),
          (0.00095, 1.4, 0.00075, 0.10, 1.0, 2.0), (0.00095, 1.45, 0.0005, 0.12, 2.0, 8.0), (0.00095, 1.4, 0.0005, 0.25, 1.2, 2.0)]
-STARTS, SHORT, LONG = 4, 350, 900
-HOW = {"B": "SS", "q0": "VV", "z0": "SS", "z1": "VV", "z2": "VV", "m0": "VV", "m1": "VV", "m2": "VV", "q1": "VV", "q2": "VV"}
+STARTS, SHORT, LONG = 4, 400, 3200
 PARTS = 4
+SETS = [(1, 0), (2, 0), (1, 1), (2, 1), (1, 2), (1, 3), (2, 2), (2, 3)]
+BLOCKS, PAIR, WSET = 6, 8192, 2064
 
 F, B, H, I, U = "float32", "bfloat16", "float16", "int32", "uint16"
 SCRATCH = {}
@@ -19,24 +20,22 @@ for _n, _w, _d in [
         ("mti", 4096, I), ("raw", 4096, I), ("wt", 4096, F), ("xw", 4096, F), ("ow", 4096, B),
         ("wd", 16, I), ("bki", 8, I), ("qsi", 24, I), ("qci", 24, I), ("pi", 8, I), ("ix", 24, F),
         ("qg", 128, F), ("qm", 128, F), ("pg", 128, F), ("c16", 32, F), ("io640", 640, F), ("c8", 8, F),
-        ("blk", 128, B), ("eqm", 128, B), ("i128", 128, B), ("jb", 16, B), ("jj", 2048, B), ("nj", 128, B),
-        ("blkp", 128, B), ("tmp", 256, B), ("tmb", 128, B), ("pmx", 128, B), ("blkpp", 128, B), ("blki", 128, B),
+        ("blk", 128, B), ("eqm", 128, B), ("i128", 128, B), ("idf", 128, F), ("jb", 16, B), ("jj", 2048, B), ("nj", 128, B),
+        ("blkp", 128, B), ("tmp", 256, B), ("tmb", 128, B), ("pmx", 128, B), ("blkpp", 128, B), ("blki", 128, B), ("cst", 128, B),
         ("zb", 248, B), ("b8f", 16, F), ("keep", 384, B), ("cole", 16, F), ("nlneg", 8, H), ("npm", 8, F), ("cnp", 8, F),
         ("neg1", 384, F), ("z8", 8, F), ("c15", 16, B),
         ("wdf", 24, F), ("dd", 512, B), ("wrb", 512, B), ("dm", 128, B), ("msk", 128, B),
-        ("sel", 9 * 2048, B), ("st", 512, B), ("sf", 4096, F), ("qcl", 24, U), ("lrow", 384, F), ("lm", 384, B), ("qsf", 24, F), ("bkl", 8, U),
+        ("sel", PAIR + BLOCKS * WSET, B), ("st", 256, B), ("qcl", 24, U), ("lrow", 384, F), ("lm", 384, B), ("qsf", 24, F), ("bkl", 8, U),
         ("ki", 8, I), ("kl", 8, U), ("qgt", 128, H), ("ql", 8, U), ("xi", 128, F), ("xl0", 128, U), ("xl1", 128, U), ("xk", 640, F),
-        ("y0", 2048, H), ("y1", 2048, H), ("y2", 2048, H), ("gf", 2048, F),
-        ("g30", 1024, H), ("g31", 1024, H), ("g32", 1024, H), ("g33", 1024, H),
-        ("g40", 1024, B), ("g41", 1024, B), ("g42", 1024, B), ("g43", 1024, B), ("gt", 2048, B),
-        ("l30", 128, U), ("l31", 128, U), ("l32", 128, U), ("lm3", 128, U),
-        ("l40", 128, U), ("l41", 128, U), ("l42", 128, U), ("l43", 128, U),
-        ("pz0", 512, F), ("pz1", 512, F), ("pz2", 512, F), ("pzn", 640, F), ("rr", 512, B), ("rn", 640, B), ("invn", 512, B),
+        ("y0", 2048, H), ("y1", 2048, H), ("y2", 2048, H), ("y3", 2048, H), ("g3", 8192, H), ("g4", 8192, B), ("gt", 2048, B),
+        ("l30", 128, U), ("l31", 128, U), ("l32", 128, U), ("l33", 128, U), ("lm3", 128, U),
+        ("l40", 128, U), ("l41", 128, U), ("l42", 128, U), ("l43", 128, U), ("l44", 128, U),
+        ("pz0", 512, F), ("pz1", 512, F), ("pz2", 512, F), ("pzn", 640, F), ("rr", 512, B), ("rn", 640, B), ("invn", 512, B), ("an", 256, B),
         ("r2", 384, B), ("rq2", 128, B), ("lhb", 1024, B),
         ("sc", 3072, F), ("nn", 8, F), ("vl", 8, F), ("uu", 8, H), ("inc", 8, H), ("ww", 8, H), ("mn", 8, H), ("ml", 8, U), ("cnt", 4, H),
         ("pl", 24, U), ("num", 512, F), ("ymt", 384, F), ("inv", 128, B),
         ("aq", 128, B), ("ne", 128, B), ("sm", 8, F), ("dd2", 16, B), ("oh", 4, F), ("ws", 4, B),
-        ("mk", 8, F), ("ya", 16, F), ("pw", 512, H), ("lw", 32, U), ("gw", 512, H), ("lw2", 32, U),
+        ("mk", 16, F), ("ya", 16, F), ("pw", 512, H), ("lw", 32, U), ("gw", 512, H), ("lw2", 32, U),
         ("gz0", 512, B), ("gz1", 512, B), ("gz2", 512, B), ("yrt", 512, F)]:
     SCRATCH[_n] = ("sbuf", [128, _w], _d)
 PSUM = ["pa0", "pa1", "pb0", "pb1", "pc0", "pc1", "pd0", "pe0"]
@@ -131,13 +130,13 @@ def plan(ops):
         elif k == STARTS * SHORT:
             cur = top
         if cur is None:
-            pr, al = prio, [0.6] * n
+            pr, al = prio, [0.4] * n
         else:
             amp = [0.5, 2.0, 6.0, 15.0][k % 4]
             frac = [0.003, 0.01, 0.03, 0.1][(k // 4) % 4]
             x, y, z = rng.rand(n).tolist(), rng.rand(n).tolist(), rng.rand(n).tolist()
             pr = [cur[2][i] + (amp * (x[i] - 0.5) if y[i] < frac else 0.0) for i in range(n)]
-            al = [(0.45 + 0.4 * z[i] if y[i] < frac else cur[3][i]) for i in range(n)]
+            al = [(0.25 + 0.75 * z[i] if y[i] < frac else cur[3][i]) for i in range(n)]
         beg, fin = place(ops, pre, succ, pr, al, durs, hop)
         b2, f2 = place(ops, succ, pre, fin, al, durs, hop, True)
         beg, fin = place(ops, pre, succ, f2, al, durs, hop)
@@ -281,8 +280,12 @@ def rank_program(g, core, T, topo):
     def move(out, in_, idx=None):
         do({"S": a_act(out, in_, idx=idx), "V": a_cp(out, in_, idx)}, [in_] + lst(idx), [out])
 
-    def scale(out, in_, col, free=False):
-        do({"S": a_act(out, in_, col), "V": a_ts(out, in_, col, OP.mult)}, [in_, col], [out], free)
+    def scale(out, in_, col, free=False, idx=None):
+        do({"S": a_act(out, in_, col, idx=idx), "V": a_ts(out, in_, col, OP.mult, idx=idx)}, [in_, col] + lst(idx), [out], free)
+
+    def step(out, idx):
+        do({"S": a_act(out, xw, 0.0625, -2048.0, idx=idx), "V": a_ts(out, xw, 0.0625, OP.mult, -2048.0, OP.add, idx=idx)},
+           [xw, idx], [out])
 
     def mms(out, pairs, f=1, parts=1):
         n = len(pairs)
@@ -351,6 +354,7 @@ def rank_program(g, core, T, topo):
     tt(view("i128"), view("eqm"), view("blk"), OP.mult)
     ts(view("b8f", 0, 8), view("pg", 0, 8), G_, OP.is_equal)
     ts(view("b8f", 8, 16), view("b8f", 0, 8), -2048.0, OP.mult)
+    move(view("idf"), view("i128"))
     cp(view("wdf", 0, 16), view("wd"))
     ts(view("wdf", 16, 20), view("wdf", 0, 16, 4), 16.0, OP.mult, 1.0, OP.add)
     tt(view("wdf", 20, 24), view("wdf", 16, 20), view("wdf", 1, 16, 4), OP.add)
@@ -360,34 +364,34 @@ def rank_program(g, core, T, topo):
     mms(view("pa0"), [(view("blk"), view("dd"))])
     act(view("wrb"), view("pa0"))
     for k in range(8):
-        c = 4 * (k % 4) + 2 + k // 4
+        c = 4 * SETS[k][1] + 1 + SETS[k][0]
         scale(view("dm", 16 * k, 16 * k + 16), view("eqm", 0, 16), view("wdf", c, c + 1))
     mms(view("pa1", 0, 128), [(view("blk"), view("dm"))])
     ts(view("msk"), view("pa1", 0, 128), A_, OP.is_equal)
 
+    def block(kind, s):
+        return PAIR + WSET * SETS.index((kind, s))
+
     def sel(kind, s, i, w=128):
-        c = 2048 + 384 * i + 128 * (s - 1) if kind == 0 and s else 2048 * (4 * kind + s) + 128 * i
+        if kind:
+            c = block(kind, s) + 128 * i
+        else:
+            c = 2048 + 384 * i + 128 * (s - 1) if s else 128 * i
         return view("sel", c, c + w)
 
     def build0(s, w):
         for i in range(16):
             ts(sel(0, s, i, w), view("wrb", 128 * s, 128 * s + w), view("cole", i, i + 1), OP.is_equal, free=True)
 
-    def selF(s, i, w=128):
-        return view("sf", 2048 * s + 128 * i, 2048 * s + 128 * i + w)
-
-    def spread(v, m, st):
+    def spread(buf, lo, hi, first, last, st):
         for k in range(8):
-            scale(view(v[1], v[2] + (16 * k if st == 129 else k), v[3], st), view("msk", m, m + 16), view("b8f", k, k + 1), free=True)
+            scale(view(buf, first(k), last(k), st), view("msk", 16 * lo, 16 * hi), view("b8f", k, k + 1), free=True)
 
-    def buildF(s):
-        spread(selF(s, 0, 2048), 16 * s, 129)
+    def build(lo, hi):
+        spread("sel", lo, hi, lambda k: PAIR + WSET * lo + 16 * k, lambda k: PAIR + WSET * (hi - 1) + 129 * 15 + 16 * k + 1, 129)
 
-    def build(kind, s):
-        spread(sel(kind, s, 0, 2048), 16 * (4 * (kind - 1) + s), 129)
-
-    def buildT(s):
-        spread(view("st", 128 * s, 128 * s + 128), 16 * (4 + s), 8)
+    def buildS():
+        spread("st", BLOCKS, 8, lambda k: k, lambda k: 256, 8)
 
     def jj(i):
         return view("jj", 128 * i, 128 * i + 128)
@@ -396,14 +400,15 @@ def rank_program(g, core, T, topo):
         chain("G", iota(v, [[0, v[4]]], c))
 
     def zero(k):
-        const(view("sel", 2048 * k, 2048 * k + 2048))
+        const(view("sel", PAIR + WSET * k, PAIR + WSET * k + 2048))
     fill(view("jj"), 0.0)
-    const(selF(0, 0, 2048))
-    zero(4)
-    zero(8)
-    const(selF(1, 0, 2048))
+    zero(0)
+    zero(1)
     const(view("neg1"), -1)
-    zero(5)
+    for k in range(2, BLOCKS):
+        zero(k)
+    const(view("rn"), -1)
+    const(view("pzn"))
     fill(view("jb"), 1.0)
     for k in range(8):
         scale(view("jj", 16 * k, 2048, 129), view("jb"), view("b8f", k, k + 1), free=True)
@@ -416,25 +421,22 @@ def rank_program(g, core, T, topo):
     fill(view("xk", 128, 640), 0.0)
     fill(view("cnt", 0, 1), 128.0)
     build0(0, 128)
-    build(1, 0)
+    build(0, 2)
 
     for h in range(NCH):
         a, b = c0[h], c0[h] + CWS[h]
         ts(view("wt", a, b), view("raw", a, b), -7.5, OP.add, C27, OP.add)
-        act(view("xw", a, b), view("wt", a, b), scale=0.0625, bias=-C27 / 16)
+        act(view("xw", a, b), view("wt", a, b), bias=-C27)
+
+    def x16(bank, x):
+        do({"S": a_act(bank, x), "P": (lambda e: e.matmul(bank[0], T.idf[:], x[0], True, True), (0, 0, 0, 4 * x[4]))},
+           [x, view("idf")], [bank])
     for k in range(8):
         a = 512 * k
         bank = view(("pc0", "pc1", "pb0", "pb1")[k % 4])
-        act(bank, view("wt", a, a + 512), bias=-C27)
+        x16(bank, view("xw", a, a + 512))
         tt(view("ow", a, a + 512), view("raw", a, a + 512), bank, OP.subtract)
-    zero(6)
-    zero(7)
-    const(view("rn"), -1)
-    const(view("pzn"))
-    buildF(0)
-    build(2, 0)
-    build(1, 1)
-    buildT(1)
+    iota(view("cst"), [[16, 16], [0, 8]], 1)
 
     def consts():
         ts(PI1, PI_, 1.0, OP.add)
@@ -449,6 +451,9 @@ def rank_program(g, core, T, topo):
         ts(view("blki"), view("pg"), G_, OP.is_equal)
         ts(view("blkpp"), view("pg"), PG_, OP.is_equal)
         ts(view("blkp"), view("qg"), PG_, OP.is_equal)
+        ts(view("cst"), view("cst"), A_, OP.add)
+        tt(view("cst"), view("cst"), view("blki"), OP.mult)
+        ts(view("cst"), view("cst"), -1.0, OP.add)
         ts(view("tmp", 0, 128), view("qm"), PI1, OP.is_equal)
         tt(view("pmx"), view("tmp", 0, 128), view("blkp"), OP.mult)
         ts(view("tmp", 128, 256), view("qm"), PI1, OP.is_gt, -1.0, OP.add)
@@ -467,8 +472,9 @@ def rank_program(g, core, T, topo):
     rot = {"g3": 0, "g4": 0}
 
     def buf(kind):
+        k = 1024 * (rot[kind] % 8)
         rot[kind] += 1
-        return view("%s%d" % (kind, rot[kind] % 4))
+        return view(kind, k, k + 1024)
 
     def pl(t):
         return view("pl", 8 * t, 8 * t + 8)
@@ -487,56 +493,46 @@ def rank_program(g, core, T, topo):
 
     def pass1(b):
         lst_ = view("bkl") if b == 0 else view("ql")
-        cp(view("xl%d" % (b % 2)), xw, idx=lst_)
-        ts(view("xk", 0, 128) if b == 0 else view("xi"), xw, -2048.0, OP.add, idx=lst_)
+        ts(view("xl%d" % (b % 2)), xw, 0.0625, OP.mult, idx=lst_)
+        step(view("xk", 0, 128) if b == 0 else view("xi"), lst_)
 
     def pass2(b):
         for h in (0, 1):
-            ts(view("y%d" % (b % 3), 1024 * h, 1024 * h + 1024), xw, -2048.0, OP.add, idx=view("xl%d" % (b % 2), 64 * h, 64 * h + 64))
+            step(view("y%d" % b, 1024 * h, 1024 * h + 1024), view("xl%d" % (b % 2), 64 * h, 64 * h + 64))
 
     def psel_x(b, out):
         for h in (0, 1):
             bank = view("pa%d" % h, 0, 64)
-            mms(bank, [(sel(0, 0, a), view("y%d" % (b % 3), 1024 * h + a, 1024 * h + 1024, 16)) for a in range(16)])
+            mms(bank, [(sel(0, 0, a), view("y%d" % b, 1024 * h + a, 1024 * h + 1024, 16)) for a in range(16)])
             ts(view(out, 64 * h, 64 * h + 64), bank, 2048.0, OP.add)
 
-    def psel_z(b, z):
-        bank = view("pe0", 0, 128)
-        mms(bank, [(sel(0, 1 + z, a), view("y%d" % (b % 3), a, 2048, 16)) for a in range(16)], 1, PARTS)
-        move(view("pz%d" % z, 128 * b, 128 * b + 128), bank)
+    def psel_z(b, z, n=1):
+        for k in range(n):
+            mms(view("pe0", 128 * k, 128 * k + 128), [(sel(0, 1 + z, a), view("y%d" % (b + k), a, 2048, 16)) for a in range(16)], 1, PARTS)
+        move(view("pz%d" % z, 128 * b, 128 * b + 128 * n), view("pe0", 0, 128 * n))
 
-    def p3(s, src, out, who):
-        how = HOW[who]
+    def p3(s, src, out, slow=False):
         for h in (0, 1):
-            idx = view(src, 64 * h, 64 * h + 64)
-            bank = view("pa%d" % h, 0, 64)
-            res = view(out, 64 * h, 64 * h + 64)
-            if how[h] == "V":
-                g3 = buf("g3")
-                ts(g3, xw, -2048.0, OP.add, idx=idx)
-                mms(bank, [(sel(1, s, e), view(g3[1], e, 1024, 16)) for e in range(16)])
-                ts(res, bank, 2048.0, OP.add)
-            else:
-                if how == "SS":
-                    bank = view("pe0", 64 * h, 64 * h + 64)
-                act(view("gf", 1024 * h, 1024 * h + 1024), xw, idx=idx)
-                mms(bank, [(selF(s, e), view("gf", 1024 * h + e, 1024 * h + 1024, 16)) for e in range(16)], 4, PARTS)
-                cp(res, bank)
+            bank = view("pe0", 256 + 64 * h, 320 + 64 * h) if slow else view("pa%d" % h, 0, 64)
+            g3 = buf("g3")
+            step(g3, view(src, 64 * h, 64 * h + 64))
+            mms(bank, [(sel(1, s, e), view("g3", g3[2] + e, g3[3], 16)) for e in range(16)])
+            ts(view(out, 64 * h, 64 * h + 64), bank, 2048.0, OP.add)
 
     def p4g(h, src):
         g4 = buf("g4")
         move(g4, ow, idx=view(src, 64 * h, 64 * h + 64))
         return g4
 
-    def p4s(h, g4, extra=(), skip=0):
+    def p4s(h, g4, extra=(), skip=-1, s=0):
         bank = view("pb%d" % h, 0, 64)
-        mms(bank, [(sel(2, 0, e), view(g4[1], e, 1024, 16)) for e in range(skip, 16)] + list(extra))
+        mms(bank, [(sel(2, s, e), view("g4", g4[2] + e, g4[3], 16)) for e in range(16) if e != skip] + list(extra))
         return bank
 
     def p4z(s, src):
         for h in (0, 1):
             move(view("gt", 1024 * h, 1024 * h + 1024), ow, idx=view(src, 64 * h, 64 * h + 64))
-        bank, m = view("pb%d" % (s % 2), 0, 128), 128 * s
+        bank, m = view("pb%d" % (s % 2), 0, 128), 128 * (s - 2)
 
         def fn(e):
             for k in range(16):
@@ -550,16 +546,15 @@ def rank_program(g, core, T, topo):
 
     def compare(t):
         b, L = t + 1, 128 * (t + 1)
+        q = view("rr", 128 * b, 128 * b + 128)
         act(view("r2", 0, L), view("rr", 0, L), scale=32.0, func=AF.Square)
-        for hh in (0, 1):
-            q = view("rr", 128 * b + 64 * hh, 128 * b + 64 * hh + 64)
-            act(view("rq2", 64 * hh, 64 * hh + 64), q, scale=32.0, func=AF.Square)
-            for k in range(8):
-                scale(view("lhb", 512 * hh + k, 512 * hh + 512, 8), q, view("b8f", 8 + k, 9 + k), free=True)
-            for c in range(4 * hh, 4 * hh + 4):
-                bank = view("pc%d" % (c % 2), 0, L)
-                mms(bank, [(view("blki"), view("r2", 0, L)), (view("lhb", 128 * c, 128 * c + 128), view("rr", 0, L))])
-                scan(view("sc", 384 * c, 384 * c + L), bank, view("neg1", 0, L), 8000000.0, OP.min, OP.add)
+        act(view("rq2"), q, scale=32.0, func=AF.Square)
+        for k in range(8):
+            scale(view("lhb", k, 1024, 8), q, view("b8f", 8 + k, 9 + k), free=True)
+        for c in range(8):
+            bank = view(("pc0", "pc1", "pa1")[c % 3], 0, L)
+            mms(bank, [(view("blki"), view("r2", 0, L)), (view("lhb", 128 * c, 128 * c + 128), view("rr", 0, L))])
+            scan(view("sc", 384 * c, 384 * c + L), bank, view("neg1", 0, L), 8000000.0, OP.min, OP.add)
         mms(view("pd0", 0, 8), [(view("zb", 120 - 8 * i, 248 - 8 * i), view("rq2", i, 128, 16)) for i in range(16)])
         act(view("nn"), view("pd0", 0, 8), scale=-1.0)
 
@@ -585,7 +580,10 @@ def rank_program(g, core, T, topo):
         nb = view("num", 128 * b, 128 * b + 128)
         move(nb, view("io640"), idx=pl(t))
         move(view("ymt", 128 * t, 128 * t + 128), view("num", 0, 128 * b + 128), idx=view("ml"))
-        ts(view("lm3"), view("pz%d" % t, 0, L + 128), 2048.0, OP.add, idx=view("ml"))
+        if t:
+            ts(view("lm3"), view("pz%d" % t, 0, L + 128), 2048.0, OP.add, idx=view("ml"))
+        else:
+            tt(view("ne"), view("an"), view("aq"), OP.not_equal, idx=view("ml"))
         if t < 2:
             q = view("rr", 128 * b, 128 * b + 128)
             ts(view("inv"), nb, 512.0, OP.is_ge, 16.0, OP.mult)
@@ -599,8 +597,11 @@ def rank_program(g, core, T, topo):
                 scatter(view("rn"), pl(k), view("rr", 128 * k + 128, 128 * k + 256))
 
     def winner(t):
-        dc, mx, sc = view("pd0", 48, 49), view("sm", 1, 2), view("sm", 2, 3)
-        mms(dc, [(view("ne"), view("jb", 0, 1))])
+        dc, mx, sc = view("pd0", 48, 49) if t else view("sm", 0, 1), view("sm", 1, 2), view("sm", 2, 3)
+        if t:
+            mms(dc, [(view("ne"), view("jb", 0, 1))])
+        else:
+            reduce(dc, view("ne"), OP.add)
         ts(view("dd2"), view("eqm", 0, 16), dc, OP.mult, 16.0, OP.mult)
         mms(view("pd0", 16, 32), [(view("blk"), view("dd2")), (view("blk"), view("c15"))])
         ts(sc, dc, 16.0, OP.mult, A15, OP.add)
@@ -610,19 +611,29 @@ def rank_program(g, core, T, topo):
         ts(view("ws"), view("wdf", 4 * t + 4, 4 * t + 8), oh, OP.mult)
         mms(view("pd0", 32, 36), [(view("blk"), view("ws"))])
         ts(view("mk", 2 * t, 2 * t + 2), view("pd0", 34, 36), A_, OP.is_equal)
+        ts(view("mk", 8 + t, 9 + t), view("mk", 2 * t, 2 * t + 1), 0.0625, OP.mult)
+        ts(view("mk", 12 + t, 13 + t), view("mk", 2 * t, 2 * t + 1), -2048.0, OP.mult)
+        if t == 0:
+            ts(view("mk", 15, 16), view("pd0", 32, 33), 16.0, OP.mult, view("pd0", 33, 34), OP.add)
         ts(view("ya", 4 * t, 4 * t + 4), view("pd0", 32, 36), ix(12 + t), OP.mult)
 
     def wpass(t, c0, c1, src):
         n = (c1 - c0) // 16
-        ts(view("pw", c0, c1), view(src, c0, c1), view("oh", t, t + 1), OP.mult)
+        h = (c1 - c0) // (2 if n > 16 else 1)
+        for a in range(c0, c1, h):
+            scale(view("pw", a, a + h), view(src, a, a + h), view("oh", t, t + 1))
         bank, bank2 = view("pc0", 0, n), view("pc1", 0, n)
         mms(bank, [(jj(i), view("pw", c0 + i, c1, 16)) for i in range(16)])
-        lw, lw2, gw = view("lw", 0, n), view("lw2", 0, n), view("gw", 0, c1 - c0)
+        lw, lw2 = view("lw", 0, n), view("lw2", 0, n)
         ts(lw, bank, 2048.0, OP.add)
-        ts(gw, xw, -2048.0, OP.add, view("mk", 2 * t, 2 * t + 1), OP.mult, idx=lw)
+        m16, mb = view("mk", 8 + t, 9 + t), view("mk", 12 + t, 13 + t)
+        for a in range(0, c1 - c0, h):
+            o, li = view("gw", a, a + h), view("lw", a // 16, (a + h) // 16)
+            do({"S": a_act(o, xw, m16, mb, idx=li), "V": a_ts(o, xw, -32768.0, OP.add, m16, OP.mult, idx=li)}, [xw, m16, mb, li], [o])
         mms(bank2, [(jj(i), view("gw", i, c1 - c0, 16)) for i in range(16)])
         ts(lw2, bank2, 2048.0, OP.add)
-        act(view("gz%d" % t, c0, c1), ow, scale=view("mk", 2 * t + 1, 2 * t + 2), idx=lw2)
+        for a in range(0, c1 - c0, h):
+            scale(view("gz%d" % t, c0 + a, c0 + a + h), ow, view("mk", 2 * t + 1, 2 * t + 2), idx=view("lw2", a // 16, (a + h) // 16))
 
     def rupdate(t):
         L = 128 * (t + 2)
@@ -637,59 +648,63 @@ def rank_program(g, core, T, topo):
     psel_x(0, "l30")
     pass2(1)
     psel_x(1, "l31")
-    p3(0, "l30", "l40", "B")
-    p3(0, "l31", "l41", "q0")
+    p3(0, "l30", "l40")
+    p3(0, "l31", "l41")
     build0(1, 384)
-    buildF(1)
     for b in (0, 1):
         for h in (0, 1):
             evac_r(b, h, p4s(h, p4g(h, "l4%d" % b)))
     consts()
-    psel_z(1, 0)
-    psel_z(0, 0)
+    build(2, BLOCKS)
+    buildS()
+    psel_z(0, 0, 2)
     compare(0)
-    ts(view("l32"), view("pz0", 128, 256), 2048.0, OP.add)
-    p3(1, "l32", "l42", "z0")
-    move(view("aq"), p4z(1, "l42"))
+    for b, x in ((1, 2), (0, 3)):
+        ts(view("l3%d" % x), view("pz0", 128 * b, 128 * b + 128), 2048.0, OP.add)
+        p3(1, "l3%d" % x, "l4%d" % (x if x == 2 else 4), True)
+        for h in (0, 1):
+            c = 128 * b + 64 * h
+            move(view("an", c, c + 64), p4s(h, p4g(h, "l4%d" % (x if x == 2 else 4)), s=1))
+    cp(view("aq"), view("an", 128, 256))
     for t in range(3):
         b = t + 2
         append(t)
-        p3(1 + t, "lm3", "l43", "m%d" % t)
+        if t:
+            p3(1 + t, "lm3", "l43")
         if t < 2:
             pass1(b)
             pass2(b)
             psel_x(b, "l31")
-        tt(view("ne"), p4z(1 + t, "l43"), view("aq"), OP.not_equal)
+        if t:
+            tt(view("ne"), p4z(1 + t, "l43"), view("aq"), OP.not_equal)
         winner(t)
-        if t == 0:
-            for z in (1, 2):
-                build(1, 1 + z)
-                buildT(1 + z)
         if t < 2:
-            for z in (0, 1):
+            for z in range(t, 2):
                 psel_z(b, z)
             if t == 0:
-                for bb in (1, 0):
-                    psel_z(bb, 1)
-            p3(0, "l31", "l41", "q%d" % (t + 1))
-        c1 = min(512, 128 * (t + 3))
-        wpass(t, 0, c1, "pzn" if t == 2 else "pz%d" % t)
-        if t == 1:
-            wpass(0, 384, 512, "pz0")
+                psel_z(0, 1, 2)
+            p3(0, "l31", "l41")
+        if t == 0:
+            ts(view("gz0", 0, 256), view("an"), view("oh", 0, 1), OP.mult)
+            wpass(0, 256, 384, "pz0")
+        else:
+            wpass(t, 0, 512, "pzn" if t == 2 else "pz1")
         if t == 2:
             break
         gs = [p4g(h, "l41") for h in (0, 1)]
         rupdate(t)
         for h in (0, 1):
             c = 128 * b + 64 * h
-            evac_r(b, h, p4s(h, gs[h], [(jj(k), view("gz%d" % k, c, c + 64)) for k in range(t + 1)], t + 1))
+            evac_r(b, h, p4s(h, gs[h], [(jj(t), view("gz%d" % t, c, c + 64))], t))
         if t == 0:
-            for bb in (1, 0):
-                psel_z(bb, 2)
+            ts(view("sel", 0, 2048, 16), view("cst"), view("mk", 15, 16), OP.is_equal)
+            for k in (1, 2):
+                ts(view("sel", block(k, 0), block(k, 0) + 128, 16), view("b8f", 0, 8), view("mk", k - 1, k), OP.mult)
+            psel_z(0, 2, 2)
         psel_z(b, 2)
         compare(t + 1)
         ts(view("l32"), view("pz%d" % (t + 1), 128 * b, 128 * b + 128), 2048.0, OP.add)
-        p3(2 + t, "l32", "l42", "z%d" % (t + 1))
+        p3(2 + t, "l32", "l42", True)
         move(view("aq"), p4z(2 + t, "l42"))
 
     ends = []

@@ -1,29 +1,52 @@
-import numpy as np
 from concourse.mybir import AluOpType, AxisListType, ActivationFunctionType
 
 OP = AluOpType
 AF = ActivationFunctionType
-CWS = [1024, 1024, 1024, 512, 512]
+CWS = [256, 1024, 1024, 1024, 512, 256]
 NCH = len(CWS)
+OWS = [2048, 2048]
 C27 = 201326592.0
+C23 = 12582912.0
 EPS = 0.499969482421875
-COSTS = [(0.00095, 1.45, 0.00052, 0.10, 1.0, 2.0), (0.00090, 1.1, 0.00050, 0.10, 1.0, 4.0), (0.0012, 1.9, 0.0006, 0.15, 1.3, 2.0),
-         (0.00095, 1.4, 0.00075, 0.10, 1.0, 2.0), (0.00095, 1.45, 0.0005, 0.12, 2.0, 8.0), (0.00095, 1.4, 0.0005, 0.25, 1.2, 2.0)]
-STARTS, SHORT, LONG = 4, 400, 3200
 PARTS = 4
+DIGITS = "0123456789abcdefghijklmnopqrstuvwxyzABCDEFGHIJKLMNOPQRSTUVWXYZ"
+ORDER = (
+    "1W2400083l040c020g0w060k0a0o0s203j0e3f3h2i2g2c2e2k4c7x0A3d2m"
+    "0i0E8h1Y2o7N2q2a4G8C2y2230342W322u2A0I2Y28262U2S360K0m2s2C2K"
+    "3r2I2M8j382H4p3N8d8f4i2E2O2Q7v0O8r4k1i4q4m4e2w584Q0q4K0u0U4O"
+    "4M0y0C1m0G0Q0M1u0W0S4S1k10121o4I1c161y1q0Y184U564y4w4A141e1s"
+    "1A5A1w1O1C1G3u3m1a4Y4C1K1g1I4u4W5C541E3p5y526A5c3E1Q5w3P5E4s"
+    "4g5G5a3a1M1S3t5I5O506E5K6G5Q3H603z6C3w5o5e5m5S3K1U639a5g5k5q"
+    "5s5i5W5Y423Q3S5U646c683C466S6j666I6M6a6Q3J6e6o6O6K6k709c6u6U"
+    "6W9e6g6Y6q74726m7c9g776s8Y3U9i9k6w3X786y7j407a7o7e7g9m7O9o7k"
+    "7ma23A3Z9r7S458O8K7WaW7qbm8F888H7t9saYa8aa8S8R7Q9uaha7alajaf"
+    "9wad9yb59A488m9C4a8M8I9094968W8Uamaqaub0aoas84ayawaCb2b6aAaE"
+    "aO86b88abh8Ba4baaGaIaK9E9GaSaQ9I92aUbcbiaMbObSbQbU7UbWbY5Nc0"
+    "9Kc6c89M4Ecc9Ocabobubec29Qcec4cobl7ycg8kcr9S9UbqcicA5u7YcFcC"
+    "cGbw9W9Ybsbya0bBbG8ucIdgcMdidkcKcOdB8obM98kybIbCckbKdGdmbFdC"
+    "dpcucmcQdqdEcScWcwdscUcYd07Adud3dPdwe2dzcydNdId4d6dcd9dbfsdQ"
+    "eodKdSdee4eqesdVfxdWeudY7Ce6e1ekewfueae9808xeeed8sey82fyehei"
+    "eEeReOeDeHeLeJeNeAfActfEeSfKemeW7EeUf0eYfCf4f2f8f6fcfofqfafe"
+    "kCfkfgfmfGfifM7GfWg0fYg2fIfQg4gag68zfOg87KgcgegggwgygkgigCgm"
+    "gogJgOfSgqfUlPgUlQgZh0gQgSgKgM7IhchbhCh6gsh2h4gEguhehMgGhEhg"
+    "h8gXhihkhGhmhIhohThqhKhOhshYi0gAi2huhzhxhQhUiyi4hAi6i9hWiilS"
+    "iAiailiCiEicifigkGimiGiuipjCiqiIixkBitiPiNiXiZiTj1iQiUjEiKkE"
+    "j6j2jMj8jaj4jijcjGjejkjmjgjojujwjqjsjyjIjAkakik6jKkkkojOjQk8"
+    "kukckPkUkekgjSjUjXkQkWjYk1kSkYk2kmkIkql0l3k5kskwl4lMl6kKl8la"
+    "lclelhltlulilwlklolqlylUlWlnlBlCkMlElGlJlKlYm0m2")
 SETS = [(1, 0), (2, 0), (1, 1), (2, 1), (1, 2), (1, 3), (2, 2), (2, 3)]
 BLOCKS, PAIR, WSET = 6, 8192, 2064
 
 F, B, H, I, U = "float32", "bfloat16", "float16", "int32", "uint16"
 SCRATCH = {}
 for _n, _w, _d in [
-        ("mti", 4096, I), ("raw", 4096, I), ("wt", 4096, F), ("xw", 4096, F), ("ow", 4096, B),
+        ("mti", 4096, I), ("wt", 4096, F), ("ob", 4096, B), ("xw", 4096, F), ("ow", 4096, B),
         ("wd", 16, I), ("bki", 8, I), ("qsi", 24, I), ("qci", 24, I), ("pi", 8, I), ("ix", 24, F),
         ("qg", 128, F), ("qm", 128, F), ("pg", 128, F), ("c16", 32, F), ("io640", 640, F), ("c8", 8, F),
-        ("blk", 128, B), ("eqm", 128, B), ("i128", 128, B), ("idf", 128, F), ("jb", 16, B), ("jj", 2048, B), ("nj", 128, B),
+        ("blk", 128, B), ("eqm", 128, B), ("i128", 128, B), ("jb", 16, B), ("jj", 2048, B), ("nj", 128, B),
         ("blkp", 128, B), ("tmp", 256, B), ("tmb", 128, B), ("pmx", 128, B), ("blkpp", 128, B), ("blki", 128, B), ("cst", 128, B),
-        ("zb", 248, B), ("b8f", 16, F), ("keep", 384, B), ("cole", 16, F), ("nlneg", 8, H), ("npm", 8, F), ("cnp", 8, F),
-        ("neg1", 384, F), ("z8", 8, F), ("c15", 16, B),
+        ("b16", 128, B), ("d15", 128, B), ("low", 128, B), ("zb", 248, B), ("b8f", 16, F), ("keep", 384, B), ("cole", 16, F),
+        ("nlneg", 8, H), ("npm", 8, F), ("cnp", 8, F), ("neg1", 384, F), ("z8", 8, F), ("c15", 16, B),
         ("wdf", 24, F), ("dd", 512, B), ("wrb", 512, B), ("dm", 128, B), ("msk", 128, B),
         ("sel", PAIR + BLOCKS * WSET, B), ("st", 256, B), ("qcl", 24, U), ("lrow", 384, F), ("lm", 384, B), ("qsf", 24, F), ("bkl", 8, U),
         ("ki", 8, I), ("kl", 8, U), ("qgt", 128, H), ("ql", 8, U), ("xi", 128, F), ("xl0", 128, U), ("xl1", 128, U), ("xk", 640, F),
@@ -41,115 +64,18 @@ for _n, _w, _d in [
 PSUM = ["pa0", "pa1", "pb0", "pb1", "pc0", "pc1", "pd0", "pe0"]
 for _n in PSUM:
     SCRATCH[_n] = ("psum", [128, 512], F)
-SEMAPHORES = ["cv", "cs", "cp", "cg", "sent", "dex", "dzs", "dbk", "dqs", "dqc", "dym", "dyr", "dye"] + ["dmt%d" % h for h in range(NCH)] + ["arr%d" % h for h in range(NCH)]
+SEMAPHORES = (["cv", "cs", "cp", "cg", "sent", "dex", "dzs", "dbk", "dqs", "dqc", "dym", "dyr", "dye"] + ["dmt%d" % h for h in range(NCH)]
+              + ["arr%d" % h for h in range(NCH + len(OWS))])
 CSEM = {"V": "cv", "S": "cs", "P": "cp", "G": "cg"}
 PLAN = {}
 
 
-def cost(w, c):
-    t = w[0] + c[0] * (w[1] + c[1] * w[2]) + c[2] * w[3]
-    return t + c[4] * w[4] + c[5] * w[5] if len(w) > 4 else t
-
-
-def evaluate(ops, order, c):
-    free, fin, end = {}, [0.0] * len(ops), 0.0
-    for i, q in order:
-        o = ops[i]
-        s = free.get(q, 0.0)
-        for d in o["deps"]:
-            s = max(s, fin[d] + c[3])
-        for d in o["soft"]:
-            if ops[d]["run"] != q:
-                s = max(s, fin[d] + c[3])
-        e = s + cost(o["alt"][q][1], c)
-        free[q] = e
-        fin[i] = e + o["lat"] * c[4]
-        end = max(end, fin[i])
-    return end
-
-
-def place(ops, pre, succ, pr, al, durs, hop, back=False):
-    n = len(ops)
-    pr = list(pr)
-    for i in (range(n) if back else range(n - 1, -1, -1)):
-        for s in succ[i]:
-            if pr[i] <= pr[s]:
-                pr[i] = pr[s] + 1e-6
-    line, fin, beg = {}, [0.0] * n, [0.0] * n
-    for i in sorted(range(n), key=lambda x: -pr[x]):
-        o = ops[i]
-        best = None
-        for x, q in enumerate([o["run"]] if back else o["alt"]):
-            if not back and len(o["alt"]) > 1 and ((al[i] > 0.75 and x == 0) or (0.5 < al[i] <= 0.75 and x == 1)):
-                continue
-            t = o["lat"] if back else 0.0
-            for d in pre[i]:
-                if back:
-                    y = fin[d] + (0.0 if ops[d]["run"] == q and i in ops[d]["soft"] else o["lat"] + hop)
-                else:
-                    y = fin[d] + (0.0 if ops[d]["run"] == q and d in o["soft"] else ops[d]["lat"] + hop)
-                if y > t:
-                    t = y
-            s, e = line.setdefault(q, ([], []))
-            w = durs[i][q]
-            k = len(s)
-            while k and e[k - 1] > t:
-                k -= 1
-            while k < len(s) and s[k] < max(t, e[k - 1] if k else 0.0) + w - 1e-9:
-                k += 1
-            t = max(t, e[k - 1] if k else 0.0)
-            if best is None or t + w < best[0]:
-                best = (t + w, t, q, k)
-        f, t, q, k = best
-        line[q][0].insert(k, t)
-        line[q][1].insert(k, f)
-        if not back:
-            o["run"] = q
-        fin[i] = f
-        beg[i] = t
-    return beg, fin
-
-
 def plan(ops):
-    n = len(ops)
-    c = COSTS[0]
-    hop = c[3]
-    durs = [{q: cost(o["alt"][q][1], c) for q in o["alt"]} for o in ops]
-    pre = [sorted(o["deps"] | o["soft"]) for o in ops]
-    succ = [[] for _ in range(n)]
-    for i in range(n):
-        for d in pre[i]:
-            succ[d].append(i)
-    prio = [0.0] * n
-    for i in range(n - 1, -1, -1):
-        prio[i] = min(durs[i].values()) + ops[i]["lat"] + max([prio[s] + hop for s in succ[i]] + [0.0])
-    first, top, cur = None, None, None
-    for k in range(STARTS * SHORT + LONG):
-        if k < STARTS * SHORT and k % SHORT == 0:
-            rng, cur = np.random.RandomState(4 + k // SHORT), None
-        elif k == STARTS * SHORT:
-            cur = top
-        if cur is None:
-            pr, al = prio, [0.4] * n
-        else:
-            amp = [0.5, 2.0, 6.0, 15.0][k % 4]
-            frac = [0.003, 0.01, 0.03, 0.1][(k // 4) % 4]
-            x, y, z = rng.rand(n).tolist(), rng.rand(n).tolist(), rng.rand(n).tolist()
-            pr = [cur[2][i] + (amp * (x[i] - 0.5) if y[i] < frac else 0.0) for i in range(n)]
-            al = [(0.25 + 0.75 * z[i] if y[i] < frac else cur[3][i]) for i in range(n)]
-        beg, fin = place(ops, pre, succ, pr, al, durs, hop)
-        b2, f2 = place(ops, succ, pre, fin, al, durs, hop, True)
-        beg, fin = place(ops, pre, succ, f2, al, durs, hop)
-        order = [(i, ops[i]["run"]) for i in sorted(range(n), key=lambda x: (beg[x], x))]
-        end = [evaluate(ops, order, x) for x in COSTS]
-        if first is None:
-            first = end
-        score = sum(e / f for e, f in zip(end, first)) + end[0] / first[0]
-        if cur is None or score < cur[0]:
-            cur = (score, end, f2, al, order)
-        if top is None or score < top[0]:
-            top = cur
-    return (top[0], top[1], top[4])
+    out = []
+    for k in range(0, len(ORDER), 2):
+        c = 62 * DIGITS.index(ORDER[k]) + DIGITS.index(ORDER[k + 1])
+        out.append((c // 2, list(ops[c // 2]["alt"])[c % 2]))
+    return out
 
 
 def rank_program(g, core, T, topo):
@@ -283,8 +209,11 @@ def rank_program(g, core, T, topo):
     def scale(out, in_, col, free=False, idx=None):
         do({"S": a_act(out, in_, col, idx=idx), "V": a_ts(out, in_, col, OP.mult, idx=idx)}, [in_, col] + lst(idx), [out], free)
 
+    def lin(out, in_, s, b=0.0):
+        do({"V": a_ts(out, in_, s, OP.mult, b, OP.add), "S": a_act(out, in_, s, b)}, [in_] + sca(s) + sca(b), [out])
+
     def step(out, idx):
-        do({"S": a_act(out, xw, 0.0625, -2048.0, idx=idx), "V": a_ts(out, xw, 0.0625, OP.mult, -2048.0, OP.add, idx=idx)},
+        do({"S": a_act(out, xw, 0.0625, -C23 - 2048.0, idx=idx), "V": a_ts(out, xw, 0.0625, OP.mult, -C23 - 2048.0, OP.add, idx=idx)},
            [xw, idx], [out])
 
     def mms(out, pairs, f=1, parts=1):
@@ -305,9 +234,17 @@ def rank_program(g, core, T, topo):
             fn = lambda e: e.iota(out[0], pattern, base, cm, allow_small_or_imprecise_dtypes=True)
         return do({"G": (fn, (0.13, 2 * out[4], 0, 0))}, [], [out])
 
-    dma("Y", view("wd", 0, 4), T.ex[:], "dex", 0.1)
-    dma("Y", view("wd", 4, 16), T.zs[:], "dzs", 0.1)
+    def const(v, c=0):
+        do({"G": (lambda e: e.iota(v[0], [[0, v[4]]], c, 0, allow_small_or_imprecise_dtypes=True), (0.13, 2 * v[4], 0, 0)),
+            "V": (lambda e: e.memset(v[0], float(c)), dv(v[4], two(v)))}, [], [v])
+
+    def zeros(name, c):
+        for a in range(c, c + 2048, 512):
+            const(view(name, a, a + 512))
+
     c0 = [sum(CWS[:h]) for h in range(NCH)]
+    dma("S", view("wd", 0, 4), T.ex[:], "dex", 0.1)
+    dma("S", view("wd", 4, 16), T.zs[:], "dzs", 0.1)
     for h in range(NCH):
         dma("Y", view("mti", c0[h], c0[h] + CWS[h]), T.mt[:, c0[h]:c0[h] + CWS[h]], "dmt%d" % h, 5.2 * CWS[h] / 4096)
     dma("S", view("bki"), T.bk[:], "dbk", 0.1)
@@ -319,15 +256,23 @@ def rank_program(g, core, T, topo):
     emask = topo.mask(core, dst)
     neng = len(topo.engines(core, dst))
 
-    def send(h):
-        a, b = c0[h], c0[h] + CWS[h]
-        v = view("mti", a, b)
-        i = do({"G": (lambda e: e.remote_dma(T.raw[:, a:b], v[0], T.sem["arr%d" % h], T.sem.sent, pid, rid, emask),
+    def send(out, v, us, h):
+        i = do({"G": (lambda e: e.remote_dma(out[0], v[0], T.sem["arr%d" % h], T.sem.sent, pid, rid, emask),
                       (0, 0, 0, 0, 1.0, 0 if h else 1))}, [v], [], tok=())
         chain("G", i)
-        flight(i, [view("raw", a, b)], 5.2 * CWS[h] / 4096, ("arr%d" % h, neng), 1.0)
+        flight(i, [out], us, ("arr%d" % h, neng), 1.0)
     for h in range(NCH):
-        send(h)
+        a, b = c0[h], c0[h] + CWS[h]
+        ts(view("wt", a, b), view("mti", a, b), -7.5, OP.add, C27, OP.add)
+        send(view("xw", a, b), view("wt", a, b), 5.2 * CWS[h] / 4096, h)
+    for k in range(8):
+        a = 512 * k
+        bank = view(("pc0", "pc1", "pb0", "pb1")[k % 4])
+        act(bank, view("wt", a, a + 512), bias=-C27)
+        tt(view("ob", a, a + 512), view("mti", a, a + 512), bank, OP.subtract)
+    for h in range(len(OWS)):
+        a = sum(OWS[:h])
+        send(view("ow", a, a + OWS[h]), view("ob", a, a + OWS[h]), 2.6 * OWS[h] / 4096, NCH + h)
 
     iota(view("pi", 0, 1), [[0, 1]], 0, 1)
     iota(view("qg"), [[1, 8], [0, 16]])
@@ -354,7 +299,6 @@ def rank_program(g, core, T, topo):
     tt(view("i128"), view("eqm"), view("blk"), OP.mult)
     ts(view("b8f", 0, 8), view("pg", 0, 8), G_, OP.is_equal)
     ts(view("b8f", 8, 16), view("b8f", 0, 8), -2048.0, OP.mult)
-    move(view("idf"), view("i128"))
     cp(view("wdf", 0, 16), view("wd"))
     ts(view("wdf", 16, 20), view("wdf", 0, 16, 4), 16.0, OP.mult, 1.0, OP.add)
     tt(view("wdf", 20, 24), view("wdf", 16, 20), view("wdf", 1, 16, 4), OP.add)
@@ -396,17 +340,12 @@ def rank_program(g, core, T, topo):
     def jj(i):
         return view("jj", 128 * i, 128 * i + 128)
 
-    def const(v, c=0):
-        chain("G", iota(v, [[0, v[4]]], c))
-
-    def zero(k):
-        const(view("sel", PAIR + WSET * k, PAIR + WSET * k + 2048))
-    fill(view("jj"), 0.0)
-    zero(0)
-    zero(1)
+    zeros("jj", 0)
+    zeros("sel", PAIR)
+    zeros("sel", PAIR + WSET)
     const(view("neg1"), -1)
     for k in range(2, BLOCKS):
-        zero(k)
+        zeros("sel", PAIR + WSET * k)
     const(view("rn"), -1)
     const(view("pzn"))
     fill(view("jb"), 1.0)
@@ -418,35 +357,21 @@ def rank_program(g, core, T, topo):
     ts(view("qsf"), view("qsi"), 1.0 / 16384, OP.mult)
     act(view("lrow"), view("io640"), idx=view("qcl"))
     ts(view("lm"), view("lrow"), A_, OP.is_equal)
-    fill(view("xk", 128, 640), 0.0)
-    fill(view("cnt", 0, 1), 128.0)
+    const(view("xk", 128, 640))
+    const(view("cnt", 0, 1), 128)
     build0(0, 128)
     build(0, 2)
-
-    for h in range(NCH):
-        a, b = c0[h], c0[h] + CWS[h]
-        ts(view("wt", a, b), view("raw", a, b), -7.5, OP.add, C27, OP.add)
-        act(view("xw", a, b), view("wt", a, b), bias=-C27)
-
-    def x16(bank, x):
-        do({"S": a_act(bank, x), "P": (lambda e: e.matmul(bank[0], T.idf[:], x[0], True, True), (0, 0, 0, 4 * x[4]))},
-           [x, view("idf")], [bank])
-    for k in range(8):
-        a = 512 * k
-        bank = view(("pc0", "pc1", "pb0", "pb1")[k % 4])
-        x16(bank, view("xw", a, a + 512))
-        tt(view("ow", a, a + 512), view("raw", a, a + 512), bank, OP.subtract)
     iota(view("cst"), [[16, 16], [0, 8]], 1)
 
     def consts():
-        ts(PI1, PI_, 1.0, OP.add)
-        ts(A15, A_, -1.0, OP.mult, 15.0, OP.add)
+        lin(PI1, PI_, 1.0, 1.0)
+        lin(A15, A_, -1.0, 15.0)
         for t in range(3):
             ts(ix(8 + t), A_, float(t), OP.not_equal)
             ts(ix(12 + t), A_, float(t), OP.is_equal)
         ts(ix(11), A_, 3.0, OP.is_ge)
-        fill(view("z8"), 0.0)
-        fill(view("zb"), 0.0)
+        const(view("z8"))
+        const(view("zb"))
         ts(view("zb", 120, 128), view("pg", 0, 8), G_, OP.is_equal)
         ts(view("blki"), view("pg"), G_, OP.is_equal)
         ts(view("blkpp"), view("pg"), PG_, OP.is_equal)
@@ -458,14 +383,18 @@ def rank_program(g, core, T, topo):
         tt(view("pmx"), view("tmp", 0, 128), view("blkp"), OP.mult)
         ts(view("tmp", 128, 256), view("qm"), PI1, OP.is_gt, -1.0, OP.add)
         tt(view("tmb"), view("tmp", 128, 256), view("blkp"), OP.mult)
-        ts(view("npm"), view("c8"), PI_, OP.add)
-        ts(view("cnp"), view("npm"), -511.0, OP.add)
-        ts(view("nlneg"), view("c8"), A_, OP.add)
-        ts(view("nlneg"), view("nlneg"), -1.0, OP.mult, 639.0, OP.add)
+        lin(view("npm"), view("c8"), 1.0, PI_)
+        lin(view("cnp"), view("npm"), 1.0, -511.0)
+        lin(view("sm", 4, 5), A_, -1.0, 639.0)
+        lin(view("nlneg"), view("c8"), -1.0, view("sm", 4, 5))
         tt(view("c15"), view("eqm", 0, 16), view("c16", 16, 32), OP.mult)
+        const(view("b16"), 16)
+        scale(view("d15"), view("i128"), A15)
+        lin(view("low"), view("blk"), 256.0, -256.0)
+        tt(view("low"), view("low"), view("d15"), OP.add)
         for t in range(3):
             scale(view("keep", 128 * t, 128 * t + 128), view("i128"), ix(8 + t))
-        ts(view("nj"), jj(2), -2.0, OP.mult)
+        lin(view("nj"), jj(2), -2.0)
         move(view("num", 0, 128), view("io640", 0, 128))
 
     xw, ow = view("xw"), view("ow")
@@ -487,13 +416,13 @@ def rank_program(g, core, T, topo):
         cp(view("kl"), view("ki"))
         if t:
             scatter(view("xk"), pl(t - 1), view("xi"))
-        tt(view("qgt"), view("xk"), view("lm", 128 * t, 128 * t + 128), OP.mult, idx=view("kl"))
+        tt(view("qgt"), view("xk") if t else view("xk", 0, 128), view("lm", 128 * t, 128 * t + 128), OP.mult, idx=view("kl"))
         mms(view("pa0", 0, 8), [(jj(i), view("qgt", i, 128, 16)) for i in range(16)])
         ts(view("ql"), view("pa0", 0, 8), 2048.0, OP.add)
 
     def pass1(b):
         lst_ = view("bkl") if b == 0 else view("ql")
-        ts(view("xl%d" % (b % 2)), xw, 0.0625, OP.mult, idx=lst_)
+        ts(view("xl%d" % (b % 2)), xw, 0.0625, OP.mult, -C23, OP.add, idx=lst_)
         step(view("xk", 0, 128) if b == 0 else view("xi"), lst_)
 
     def pass2(b):
@@ -511,11 +440,13 @@ def rank_program(g, core, T, topo):
             mms(view("pe0", 128 * k, 128 * k + 128), [(sel(0, 1 + z, a), view("y%d" % (b + k), a, 2048, 16)) for a in range(16)], 1, PARTS)
         move(view("pz%d" % z, 128 * b, 128 * b + 128 * n), view("pe0", 0, 128 * n))
 
-    def p3(s, src, out, slow=False):
+    def p3(s, src, out, slow=0):
         for h in (0, 1):
-            bank = view("pe0", 256 + 64 * h, 320 + 64 * h) if slow else view("pa%d" % h, 0, 64)
+            bank = view(("pa%d" % h, "pb%d" % h, "pe0")[slow], 64 * h, 64 * h + 64)
             g3 = buf("g3")
-            step(g3, view(src, 64 * h, 64 * h + 64))
+            w = 32 if slow == 2 else 64
+            for a in range(0, 64, w):
+                step(view("g3", g3[2] + 16 * a, g3[2] + 16 * (a + w)), view(src, 64 * h + a, 64 * h + a + w))
             mms(bank, [(sel(1, s, e), view("g3", g3[2] + e, g3[3], 16)) for e in range(16)])
             ts(view(out, 64 * h, 64 * h + 64), bank, 2048.0, OP.add)
 
@@ -529,9 +460,9 @@ def rank_program(g, core, T, topo):
         mms(bank, [(sel(2, s, e), view("g4", g4[2] + e, g4[3], 16)) for e in range(16) if e != skip] + list(extra))
         return bank
 
-    def p4z(s, src):
-        for h in (0, 1):
-            move(view("gt", 1024 * h, 1024 * h + 1024), ow, idx=view(src, 64 * h, 64 * h + 64))
+    def p4z(s, src, w=64):
+        for a in range(0, 128, w):
+            move(view("gt", 16 * a, 16 * (a + w)), ow, idx=view(src, a, a + w))
         bank, m = view("pb%d" % (s % 2), 0, 128), 128 * (s - 2)
 
         def fn(e):
@@ -574,7 +505,7 @@ def rank_program(g, core, T, topo):
         cp(pl(t), view("pd0", 0, 8))
         if t < 2:
             lookup(t + 1)
-            cp(view("cnt", t + 1, t + 2), view("pd0", 8, 9))
+            move(view("cnt", t + 1, t + 2), view("pd0", 8, 9))
             ts(view("cnp"), view("cnp"), view("pd0", 9, 10), OP.add)
         ts(view("ml"), view("pc0", 0, 8), float(L), OP.add)
         nb = view("num", 128 * b, 128 * b + 128)
@@ -597,25 +528,29 @@ def rank_program(g, core, T, topo):
                 scatter(view("rn"), pl(k), view("rr", 128 * k + 128, 128 * k + 256))
 
     def winner(t):
-        dc, mx, sc = view("pd0", 48, 49) if t else view("sm", 0, 1), view("sm", 1, 2), view("sm", 2, 3)
+        mx = view("sm", 1, 2)
         if t:
-            mms(dc, [(view("ne"), view("jb", 0, 1))])
+            sc = view("pd0", 48, 49)
+            mms(view("pd0", 64, 192), [(view("blk"), view("low")), (view("b16"), view("ne"))])
+            mms(sc, [(view("d15"), view("jb", 0, 1)), (view("ne"), view("b16", 0, 1))])
+            reduce(mx, view("pd0", 64, 192), OP.max)
         else:
+            dc, sc = view("sm", 0, 1), view("sm", 2, 3)
             reduce(dc, view("ne"), OP.add)
-        ts(view("dd2"), view("eqm", 0, 16), dc, OP.mult, 16.0, OP.mult)
-        mms(view("pd0", 16, 32), [(view("blk"), view("dd2")), (view("blk"), view("c15"))])
-        ts(sc, dc, 16.0, OP.mult, A15, OP.add)
-        reduce(mx, view("pd0", 16, 32), OP.max)
+            ts(view("dd2"), view("eqm", 0, 16), dc, OP.mult, 16.0, OP.mult)
+            mms(view("pd0", 16, 32), [(view("blk"), view("dd2")), (view("blk"), view("c15"))])
+            ts(sc, dc, 16.0, OP.mult, A15, OP.add)
+            reduce(mx, view("pd0", 16, 32), OP.max)
         oh = view("oh", t, t + 1)
         ts(oh, sc, mx, OP.is_equal)
-        ts(view("ws"), view("wdf", 4 * t + 4, 4 * t + 8), oh, OP.mult)
+        scale(view("ws"), view("wdf", 4 * t + 4, 4 * t + 8), oh)
         mms(view("pd0", 32, 36), [(view("blk"), view("ws"))])
         ts(view("mk", 2 * t, 2 * t + 2), view("pd0", 34, 36), A_, OP.is_equal)
-        ts(view("mk", 8 + t, 9 + t), view("mk", 2 * t, 2 * t + 1), 0.0625, OP.mult)
-        ts(view("mk", 12 + t, 13 + t), view("mk", 2 * t, 2 * t + 1), -2048.0, OP.mult)
+        lin(view("mk", 8 + t, 9 + t), view("mk", 2 * t, 2 * t + 1), 0.0625)
+        lin(view("mk", 12 + t, 13 + t), view("mk", 2 * t, 2 * t + 1), -C23 - 2048.0)
         if t == 0:
             ts(view("mk", 15, 16), view("pd0", 32, 33), 16.0, OP.mult, view("pd0", 33, 34), OP.add)
-        ts(view("ya", 4 * t, 4 * t + 4), view("pd0", 32, 36), ix(12 + t), OP.mult)
+        scale(view("ya", 4 * t, 4 * t + 4), view("pd0", 32, 36), ix(12 + t))
 
     def wpass(t, c0, c1, src):
         n = (c1 - c0) // 16
@@ -629,7 +564,7 @@ def rank_program(g, core, T, topo):
         m16, mb = view("mk", 8 + t, 9 + t), view("mk", 12 + t, 13 + t)
         for a in range(0, c1 - c0, h):
             o, li = view("gw", a, a + h), view("lw", a // 16, (a + h) // 16)
-            do({"S": a_act(o, xw, m16, mb, idx=li), "V": a_ts(o, xw, -32768.0, OP.add, m16, OP.mult, idx=li)}, [xw, m16, mb, li], [o])
+            do({"S": a_act(o, xw, m16, mb, idx=li), "V": a_ts(o, xw, -C27 - 32768.0, OP.add, m16, OP.mult, idx=li)}, [xw, m16, mb, li], [o])
         mms(bank2, [(jj(i), view("gw", i, c1 - c0, 16)) for i in range(16)])
         ts(lw2, bank2, 2048.0, OP.add)
         for a in range(0, c1 - c0, h):
@@ -657,15 +592,16 @@ def rank_program(g, core, T, topo):
     consts()
     build(2, BLOCKS)
     buildS()
-    psel_z(0, 0, 2)
+    for z in range(3):
+        psel_z(0, z, 2)
     compare(0)
     for b, x in ((1, 2), (0, 3)):
         ts(view("l3%d" % x), view("pz0", 128 * b, 128 * b + 128), 2048.0, OP.add)
-        p3(1, "l3%d" % x, "l4%d" % (x if x == 2 else 4), True)
+        p3(1, "l3%d" % x, "l4%d" % (x if x == 2 else 4), 1)
         for h in (0, 1):
             c = 128 * b + 64 * h
             move(view("an", c, c + 64), p4s(h, p4g(h, "l4%d" % (x if x == 2 else 4)), s=1))
-    cp(view("aq"), view("an", 128, 256))
+    move(view("aq"), view("an", 128, 256))
     for t in range(3):
         b = t + 2
         append(t)
@@ -681,11 +617,9 @@ def rank_program(g, core, T, topo):
         if t < 2:
             for z in range(t, 2):
                 psel_z(b, z)
-            if t == 0:
-                psel_z(0, 1, 2)
             p3(0, "l31", "l41")
         if t == 0:
-            ts(view("gz0", 0, 256), view("an"), view("oh", 0, 1), OP.mult)
+            scale(view("gz0", 0, 256), view("an"), view("oh", 0, 1))
             wpass(0, 256, 384, "pz0")
         else:
             wpass(t, 0, 512, "pzn" if t == 2 else "pz1")
@@ -700,12 +634,11 @@ def rank_program(g, core, T, topo):
             ts(view("sel", 0, 2048, 16), view("cst"), view("mk", 15, 16), OP.is_equal)
             for k in (1, 2):
                 ts(view("sel", block(k, 0), block(k, 0) + 128, 16), view("b8f", 0, 8), view("mk", k - 1, k), OP.mult)
-            psel_z(0, 2, 2)
         psel_z(b, 2)
         compare(t + 1)
         ts(view("l32"), view("pz%d" % (t + 1), 128 * b, 128 * b + 128), 2048.0, OP.add)
-        p3(2 + t, "l32", "l42", True)
-        move(view("aq"), p4z(2 + t, "l42"))
+        p3(2 + t, "l32", "l42", 2)
+        move(view("aq"), p4z(2 + t, "l42", 32))
 
     ends = []
 
@@ -714,7 +647,7 @@ def rank_program(g, core, T, topo):
         ends.append(sem)
     out(T.ym[:], T.ymt[::16, :], view("ymt"), "dym")
     yet = view("ya", 12, 16)
-    ts(yet, view("wdf", 0, 4), ix(11), OP.mult)
+    scale(yet, view("wdf", 0, 4), ix(11))
     for t in range(3):
         tt(yet, yet, view("ya", 4 * t, 4 * t + 4), OP.add)
     out(T.ye[:], T.ya[:, 12:16], yet, "dye")
@@ -722,14 +655,13 @@ def rank_program(g, core, T, topo):
     ts(view("yrt"), view("pc0"), -1.0, OP.max)
     out(T.yr[:], T.yrt[:], view("yrt"), "dyr")
 
-    if "p" not in PLAN:
-        PLAN["p"] = plan(ops)
-        PLAN["ops"] = ops
+    PLAN["ops"], PLAN["p"] = ops, plan(ops)
     pos = {q: 0 for q in queue}
     seen = {q: {} for q in queue}
-    for i, q in PLAN["p"][2]:
+    for i, q in PLAN["p"]:
+        ops[i]["run"] = q
+    for i, q in PLAN["p"]:
         o = ops[i]
-        o["run"] = q
         if q == "D":
             continue
         want = {}
@@ -748,6 +680,6 @@ def rank_program(g, core, T, topo):
             o["tok"] = (CSEM[q], pos[q])
     for s in ends:
         g.sync.wait_ge(T.sem[s], 16)
-    g.wait_ge(T.sem.sent, NCH * neng)
+    g.wait_ge(T.sem.sent, (NCH + len(OWS)) * neng)
     for q in sorted(CSEM):
         g.wait_ge(T.sem[CSEM[q]], pos[q])

from concourse.mybir import AluOpType, AxisListType, ActivationFunctionType

OP = AluOpType
AF = ActivationFunctionType
CWS = [256, 1024, 1024, 1024, 512, 256]
NCH = len(CWS)
OWS = [2048, 2048]
C27 = 201326592.0
C23 = 12582912.0
EPS = 0.499969482421875
PARTS = 4
DIGITS = "0123456789abcdefghijklmnopqrstuvwxyzABCDEFGHIJKLMNOPQRSTUVWXYZ"
ORDER = (
    "1W2400083l040c020g0w060k0a0o0s203j0e3f3h2i2g2c2e2k4c7x0A3d2m"
    "0i0E8h1Y2o7N2q2a4G8C2y2230342W322u2A0I2Y28262U2S360K0m2s2C2K"
    "3r2I2M8j382H4p3N8d8f4i2E2O2Q7v0O8r4k1i4q4m4e2w584Q0q4K0u0U4O"
    "4M0y0C1m0G0Q0M1u0W0S4S1k10121o4I1c161y1q0Y184U564y4w4A141e1s"
    "1A5A1w1O1C1G3u3m1a4Y4C1K1g1I4u4W5C541E3p5y526A5c3E1Q5w3P5E4s"
    "4g5G5a3a1M1S3t5I5O506E5K6G5Q3H603z6C3w5o5e5m5S3K1U639a5g5k5q"
    "5s5i5W5Y423Q3S5U646c683C466S6j666I6M6a6Q3J6e6o6O6K6k709c6u6U"
    "6W9e6g6Y6q74726m7c9g776s8Y3U9i9k6w3X786y7j407a7o7e7g9m7O9o7k"
    "7ma23A3Z9r7S458O8K7WaW7qbm8F888H7t9saYa8aa8S8R7Q9uaha7alajaf"
    "9wad9yb59A488m9C4a8M8I9094968W8Uamaqaub0aoas84ayawaCb2b6aAaE"
    "aO86b88abh8Ba4baaGaIaK9E9GaSaQ9I92aUbcbiaMbObSbQbU7UbWbY5Nc0"
    "9Kc6c89M4Ecc9Ocabobubec29Qcec4cobl7ycg8kcr9S9UbqcicA5u7YcFcC"
    "cGbw9W9Ybsbya0bBbG8ucIdgcMdidkcKcOdB8obM98kybIbCckbKdGdmbFdC"
    "dpcucmcQdqdEcScWcwdscUcYd07Adud3dPdwe2dzcydNdId4d6dcd9dbfsdQ"
    "eodKdSdee4eqesdVfxdWeudY7Ce6e1ekewfueae9808xeeed8sey82fyehei"
    "eEeReOeDeHeLeJeNeAfActfEeSfKemeW7EeUf0eYfCf4f2f8f6fcfofqfafe"
    "kCfkfgfmfGfifM7GfWg0fYg2fIfQg4gag68zfOg87KgcgegggwgygkgigCgm"
    "gogJgOfSgqfUlPgUlQgZh0gQgSgKgM7IhchbhCh6gsh2h4gEguhehMgGhEhg"
    "h8gXhihkhGhmhIhohThqhKhOhshYi0gAi2huhzhxhQhUiyi4hAi6i9hWiilS"
    "iAiailiCiEicifigkGimiGiuipjCiqiIixkBitiPiNiXiZiTj1iQiUjEiKkE"
    "j6j2jMj8jaj4jijcjGjejkjmjgjojujwjqjsjyjIjAkakik6jKkkkojOjQk8"
    "kukckPkUkekgjSjUjXkQkWjYk1kSkYk2kmkIkql0l3k5kskwl4lMl6kKl8la"
    "lclelhltlulilwlklolqlylUlWlnlBlCkMlElGlJlKlYm0m2")
SETS = [(1, 0), (2, 0), (1, 1), (2, 1), (1, 2), (1, 3), (2, 2), (2, 3)]
BLOCKS, PAIR, WSET = 6, 8192, 2064

F, B, H, I, U = "float32", "bfloat16", "float16", "int32", "uint16"
SCRATCH = {}
for _n, _w, _d in [
        ("mti", 4096, I), ("wt", 4096, F), ("ob", 4096, B), ("xw", 4096, F), ("ow", 4096, B),
        ("wd", 16, I), ("bki", 8, I), ("qsi", 24, I), ("qci", 24, I), ("pi", 8, I), ("ix", 24, F),
        ("qg", 128, F), ("qm", 128, F), ("pg", 128, F), ("c16", 32, F), ("io640", 640, F), ("c8", 8, F),
        ("blk", 128, B), ("eqm", 128, B), ("i128", 128, B), ("jb", 16, B), ("jj", 2048, B), ("nj", 128, B),
        ("blkp", 128, B), ("tmp", 256, B), ("tmb", 128, B), ("pmx", 128, B), ("blkpp", 128, B), ("blki", 128, B), ("cst", 128, B),
        ("b16", 128, B), ("d15", 128, B), ("low", 128, B), ("zb", 248, B), ("b8f", 16, F), ("keep", 384, B), ("cole", 16, F),
        ("nlneg", 8, H), ("npm", 8, F), ("cnp", 8, F), ("neg1", 384, F), ("z8", 8, F), ("c15", 16, B),
        ("wdf", 24, F), ("dd", 512, B), ("wrb", 512, B), ("dm", 128, B), ("msk", 128, B),
        ("sel", PAIR + BLOCKS * WSET, B), ("st", 256, B), ("qcl", 24, U), ("lrow", 384, F), ("lm", 384, B), ("qsf", 24, F), ("bkl", 8, U),
        ("ki", 8, I), ("kl", 8, U), ("qgt", 128, H), ("ql", 8, U), ("xi", 128, F), ("xl0", 128, U), ("xl1", 128, U), ("xk", 640, F),
        ("y0", 2048, H), ("y1", 2048, H), ("y2", 2048, H), ("y3", 2048, H), ("g3", 8192, H), ("g4", 8192, B), ("gt", 2048, B),
        ("l30", 128, U), ("l31", 128, U), ("l32", 128, U), ("l33", 128, U), ("lm3", 128, U),
        ("l40", 128, U), ("l41", 128, U), ("l42", 128, U), ("l43", 128, U), ("l44", 128, U),
        ("pz0", 512, F), ("pz1", 512, F), ("pz2", 512, F), ("pzn", 640, F), ("rr", 512, B), ("rn", 640, B), ("invn", 512, B), ("an", 256, B),
        ("r2", 384, B), ("rq2", 128, B), ("lhb", 1024, B),
        ("sc", 3072, F), ("nn", 8, F), ("vl", 8, F), ("uu", 8, H), ("inc", 8, H), ("ww", 8, H), ("mn", 8, H), ("ml", 8, U), ("cnt", 4, H),
        ("pl", 24, U), ("num", 512, F), ("ymt", 384, F), ("inv", 128, B),
        ("aq", 128, B), ("ne", 128, B), ("sm", 8, F), ("dd2", 16, B), ("oh", 4, F), ("ws", 4, B),
        ("mk", 16, F), ("ya", 16, F), ("pw", 512, H), ("lw", 32, U), ("gw", 512, H), ("lw2", 32, U),
        ("gz0", 512, B), ("gz1", 512, B), ("gz2", 512, B), ("yrt", 512, F)]:
    SCRATCH[_n] = ("sbuf", [128, _w], _d)
PSUM = ["pa0", "pa1", "pb0", "pb1", "pc0", "pc1", "pd0", "pe0"]
for _n in PSUM:
    SCRATCH[_n] = ("psum", [128, 512], F)
SEMAPHORES = (["cv", "cs", "cp", "cg", "sent", "dex", "dzs", "dbk", "dqs", "dqc", "dym", "dyr", "dye"] + ["dmt%d" % h for h in range(NCH)]
              + ["arr%d" % h for h in range(NCH + len(OWS))])
CSEM = {"V": "cv", "S": "cs", "P": "cp", "G": "cg"}
PLAN = {}


def plan(ops):
    out = []
    for k in range(0, len(ORDER), 2):
        c = 62 * DIGITS.index(ORDER[k]) + DIGITS.index(ORDER[k + 1])
        out.append((c // 2, list(ops[c // 2]["alt"])[c % 2]))
    return out


def rank_program(g, core, T, topo):
    rank = T.rank_of(core)
    if rank is None:
        return
    queue = {"V": g.vector, "S": g.scalar, "P": g.tensor, "G": g, "Y": g.sync, "D": None}
    ops = []
    wrote, readers = {}, {}

    def view(name, c0=0, c1=None, st=1):
        if c1 is None:
            c1 = SCRATCH[name][1][1]
        ap = T[name][:, c0:c1] if st == 1 else T[name][:, c0:c1:st]
        return (ap, name, c0, c1, (c1 - c0 + st - 1) // st)

    def do(alt, reads, writes, free=False, tok=None, lat=0.0, dep=()):
        i = len(ops)
        deps, soft = set(dep), set()
        for v in reads:
            ps = v[1] in PSUM
            for (a, b, j) in wrote.get(v[1], []):
                if a < v[3] and v[2] < b:
                    deps.add(j)
                elif ps:
                    soft.add(j)
            if ps:
                soft.update(j for (a, b, j) in readers.get(v[1], []))
        for v in writes:
            ps = v[1] in PSUM
            for (a, b, j) in wrote.get(v[1], []):
                if ps:
                    soft.add(j)
                elif a < v[3] and v[2] < b and not (free and ops[j]["free"]):
                    deps.add(j)
            for (a, b, j) in readers.get(v[1], []):
                if a < v[3] and v[2] < b:
                    deps.add(j)
                elif ps:
                    soft.add(j)
        ops.append({"alt": alt, "lat": lat, "deps": deps, "soft": soft - deps, "tok": tok, "free": free, "run": None,
                    "nm": writes[0][1] if writes else "-"})
        for v in writes:
            if not free:
                for d in (wrote, readers):
                    d[v[1]] = [r for r in d.get(v[1], []) if not (v[2] <= r[0] and r[1] <= v[3])]
            wrote.setdefault(v[1], []).append((v[2], v[3], i))
        for v in reads:
            readers.setdefault(v[1], []).append((v[2], v[3], i))
        return i

    chains = {}

    def chain(q, i):
        if q in chains:
            ops[i]["soft"].add(chains[q])
        chains[q] = i

    def flight(i, out, us, tok, lat):
        j = do({"D": (None, (0, 0, 0, 0, us, 0))}, [], out, tok=tok, lat=lat, dep=[i])
        chain("D", j)

    def dma(q, out, in_ap, sem, us):
        i = do({q: (lambda e: e.dma_start(out[0], in_ap).then_inc(T.sem[sem], 16), (0.1, 0, 0, 0))}, [], [], tok=())
        chain(q, i)
        flight(i, [out], us, (sem, 16), 2.0)

    def sca(s):
        return [s] if isinstance(s, tuple) else []

    def val(s):
        return s[0] if isinstance(s, tuple) else s

    def two(*vs):
        return all(SCRATCH[v[1]][2] in (B, H, U) for v in vs)

    def dv(n, half=False):
        return (0.03, max(64, n * (0.5 if half else 1.0)), 0, 0)

    def ind(v, idx):
        return v[0] if idx is None else v[0].indirect(idx[0])

    def lst(idx):
        return [] if idx is None else [idx]

    def a_ts(out, in0, s1, op0, s2=None, op1=None, idx=None):
        i0 = ind(in0, idx)
        w = dv(out[4], two(out, in0)) if idx is None else (0.05, 0, out[4], 0)
        if op1 is None:
            return (lambda e: e.tensor_scalar(out[0], i0, val(s1), None, op0), w)
        return (lambda e: e.tensor_scalar(out[0], i0, val(s1), val(s2), op0, op1), w)

    def a_act(out, in_, scale=1.0, bias=0.0, func=AF.Identity, idx=None):
        i0 = ind(in_, idx)
        return (lambda e: e.activation(out[0], i0, func, bias=val(bias), scale=val(scale)),
                (0.065, 0, out[4], 0) if idx else (0.065, out[4], 0, 0))

    def a_cp(out, in_, idx=None):
        i0 = ind(in_, idx)
        return (lambda e: e.tensor_copy(out[0], i0), dv(out[4], two(out, in_)) if idx is None else (0.05, 0, out[4], 0))

    def ts(out, in0, s1, op0, s2=None, op1=None, free=False, idx=None):
        do({"V": a_ts(out, in0, s1, op0, s2, op1, idx)}, [in0] + sca(s1) + sca(s2) + lst(idx), [out], free)

    def tt(out, in0, in1, op, idx=None):
        i0 = ind(in0, idx)
        w = (0.05, 0, out[4], 0) if idx else dv(out[4] * (1 if in0[1] in PSUM or in1[1] in PSUM else 2))
        do({"V": (lambda e: e.tensor_tensor(out[0], i0, in1[0], op), w)}, [in0, in1] + lst(idx), [out])

    def cp(out, in_, idx=None):
        do({"V": a_cp(out, in_, idx)}, [in_] + lst(idx), [out])

    def fill(out, c):
        do({"V": (lambda e: e.memset(out[0], c), dv(out[4], two(out)))}, [], [out])

    def scatter(win, idx, in_):
        do({"V": (lambda e: e.tensor_copy(win[0].indirect(idx[0]), in_[0]), (0.05, 0, 2 * in_[4], 0))}, [in_, idx], [win])

    def scan(out, d0, d1, init, op0, op1):
        do({"V": (lambda e: e.tensor_tensor_scan(out[0], d0[0], d1[0], init, op0, op1), dv(out[4]))}, [d0, d1], [out])

    def reduce(out, in_, op):
        do({"V": (lambda e: e.tensor_reduce(out[0], in_[0], AxisListType.X, op), dv(in_[4]))}, [in_], [out])

    def act(out, in_, scale=1.0, bias=0.0, func=AF.Identity, idx=None):
        do({"S": a_act(out, in_, scale, bias, func, idx)}, [in_] + sca(scale) + sca(bias) + lst(idx), [out])

    def move(out, in_, idx=None):
        do({"S": a_act(out, in_, idx=idx), "V": a_cp(out, in_, idx)}, [in_] + lst(idx), [out])

    def scale(out, in_, col, free=False, idx=None):
        do({"S": a_act(out, in_, col, idx=idx), "V": a_ts(out, in_, col, OP.mult, idx=idx)}, [in_, col] + lst(idx), [out], free)

    def lin(out, in_, s, b=0.0):
        do({"V": a_ts(out, in_, s, OP.mult, b, OP.add), "S": a_act(out, in_, s, b)}, [in_] + sca(s) + sca(b), [out])

    def step(out, idx):
        do({"S": a_act(out, xw, 0.0625, -C23 - 2048.0, idx=idx), "V": a_ts(out, xw, 0.0625, OP.mult, -C23 - 2048.0, OP.add, idx=idx)},
           [xw, idx], [out])

    def mms(out, pairs, f=1, parts=1):
        n = len(pairs)
        for m in range(parts):
            lo, hi = n * m // parts, n * (m + 1) // parts

            def fn(e, lo=lo, hi=hi):
                for k in range(lo, hi):
                    r = e.matmul(out[0], pairs[k][0][0], pairs[k][1][0], k == 0, k == n - 1)
                return r
            do({"P": (fn, (0, 0, 0, f * (hi - lo) * max(64, out[4])))}, [p for pr in pairs[lo:hi] for p in pr], [out])

    def iota(out, pattern, base=0, cm=0):
        if out[1] == "pi":
            fn = lambda e: e.iota(out[0], pattern, base, cm)
        else:
            fn = lambda e: e.iota(out[0], pattern, base, cm, allow_small_or_imprecise_dtypes=True)
        return do({"G": (fn, (0.13, 2 * out[4], 0, 0))}, [], [out])

    def const(v, c=0):
        do({"G": (lambda e: e.iota(v[0], [[0, v[4]]], c, 0, allow_small_or_imprecise_dtypes=True), (0.13, 2 * v[4], 0, 0)),
            "V": (lambda e: e.memset(v[0], float(c)), dv(v[4], two(v)))}, [], [v])

    def zeros(name, c):
        for a in range(c, c + 2048, 512):
            const(view(name, a, a + 512))

    c0 = [sum(CWS[:h]) for h in range(NCH)]
    dma("S", view("wd", 0, 4), T.ex[:], "dex", 0.1)
    dma("S", view("wd", 4, 16), T.zs[:], "dzs", 0.1)
    for h in range(NCH):
        dma("Y", view("mti", c0[h], c0[h] + CWS[h]), T.mt[:, c0[h]:c0[h] + CWS[h]], "dmt%d" % h, 5.2 * CWS[h] / 4096)
    dma("S", view("bki"), T.bk[:], "dbk", 0.1)
    dma("S", view("qci"), T.qc[:], "dqc", 0.1)
    dma("S", view("qsi"), T.qs[:], "dqs", 0.1)

    dst = T.cores[(rank - 1) % len(T.cores)]
    rid, pid, _ = topo.addr(dst)
    emask = topo.mask(core, dst)
    neng = len(topo.engines(core, dst))

    def send(out, v, us, h):
        i = do({"G": (lambda e: e.remote_dma(out[0], v[0], T.sem["arr%d" % h], T.sem.sent, pid, rid, emask),
                      (0, 0, 0, 0, 1.0, 0 if h else 1))}, [v], [], tok=())
        chain("G", i)
        flight(i, [out], us, ("arr%d" % h, neng), 1.0)
    for h in range(NCH):
        a, b = c0[h], c0[h] + CWS[h]
        ts(view("wt", a, b), view("mti", a, b), -7.5, OP.add, C27, OP.add)
        send(view("xw", a, b), view("wt", a, b), 5.2 * CWS[h] / 4096, h)
    for k in range(8):
        a = 512 * k
        bank = view(("pc0", "pc1", "pb0", "pb1")[k % 4])
        act(bank, view("wt", a, a + 512), bias=-C27)
        tt(view("ob", a, a + 512), view("mti", a, a + 512), bank, OP.subtract)
    for h in range(len(OWS)):
        a = sum(OWS[:h])
        send(view("ow", a, a + OWS[h]), view("ob", a, a + OWS[h]), 2.6 * OWS[h] / 4096, NCH + h)

    iota(view("pi", 0, 1), [[0, 1]], 0, 1)
    iota(view("qg"), [[1, 8], [0, 16]])
    iota(view("qm"), [[0, 8], [1, 16]], 1)
    iota(view("c16", 0, 16), [[16, 16]], 1)
    iota(view("pg"), [[0, 16], [1, 8]])
    iota(view("c8"), [[16, 8]])
    iota(view("c16", 16, 32), [[-1, 16]], 15)
    iota(view("io640"), [[1, 640]])
    pi = view("pi", 0, 1)
    ts(view("pi", 4, 5), pi, 15, OP.bitwise_and)
    ts(view("pi", 5, 6), pi, 4, OP.arith_shift_right)
    ts(view("pi", 6, 7), pi, 7, OP.bitwise_and)
    ts(view("pi", 7, 8), pi, 3, OP.arith_shift_right)
    cp(view("ix", 0, 4), view("pi", 4, 8))

    def ix(k):
        return view("ix", k, k + 1)
    A_, G_, PG_, PI_ = ix(0), ix(1), ix(2), ix(3)
    A1, PI1, A15 = ix(4), ix(5), ix(7)
    ts(A1, A_, 1.0, OP.add)
    ts(view("blk"), view("qg"), G_, OP.is_equal)
    ts(view("eqm"), view("qm"), A1, OP.is_equal)
    tt(view("i128"), view("eqm"), view("blk"), OP.mult)
    ts(view("b8f", 0, 8), view("pg", 0, 8), G_, OP.is_equal)
    ts(view("b8f", 8, 16), view("b8f", 0, 8), -2048.0, OP.mult)
    cp(view("wdf", 0, 16), view("wd"))
    ts(view("wdf", 16, 20), view("wdf", 0, 16, 4), 16.0, OP.mult, 1.0, OP.add)
    tt(view("wdf", 20, 24), view("wdf", 16, 20), view("wdf", 1, 16, 4), OP.add)
    ts(view("cole"), view("c16", 0, 16), A_, OP.add)
    for k in range(4):
        scale(view("dd", 128 * k, 128 * k + 128), view("i128"), view("wdf", 20 + k, 21 + k))
    mms(view("pa0"), [(view("blk"), view("dd"))])
    act(view("wrb"), view("pa0"))
    for k in range(8):
        c = 4 * SETS[k][1] + 1 + SETS[k][0]
        scale(view("dm", 16 * k, 16 * k + 16), view("eqm", 0, 16), view("wdf", c, c + 1))
    mms(view("pa1", 0, 128), [(view("blk"), view("dm"))])
    ts(view("msk"), view("pa1", 0, 128), A_, OP.is_equal)

    def block(kind, s):
        return PAIR + WSET * SETS.index((kind, s))

    def sel(kind, s, i, w=128):
        if kind:
            c = block(kind, s) + 128 * i
        else:
            c = 2048 + 384 * i + 128 * (s - 1) if s else 128 * i
        return view("sel", c, c + w)

    def build0(s, w):
        for i in range(16):
            ts(sel(0, s, i, w), view("wrb", 128 * s, 128 * s + w), view("cole", i, i + 1), OP.is_equal, free=True)

    def spread(buf, lo, hi, first, last, st):
        for k in range(8):
            scale(view(buf, first(k), last(k), st), view("msk", 16 * lo, 16 * hi), view("b8f", k, k + 1), free=True)

    def build(lo, hi):
        spread("sel", lo, hi, lambda k: PAIR + WSET * lo + 16 * k, lambda k: PAIR + WSET * (hi - 1) + 129 * 15 + 16 * k + 1, 129)

    def buildS():
        spread("st", BLOCKS, 8, lambda k: k, lambda k: 256, 8)

    def jj(i):
        return view("jj", 128 * i, 128 * i + 128)

    zeros("jj", 0)
    zeros("sel", PAIR)
    zeros("sel", PAIR + WSET)
    const(view("neg1"), -1)
    for k in range(2, BLOCKS):
        zeros("sel", PAIR + WSET * k)
    const(view("rn"), -1)
    const(view("pzn"))
    fill(view("jb"), 1.0)
    for k in range(8):
        scale(view("jj", 16 * k, 2048, 129), view("jb"), view("b8f", k, k + 1), free=True)

    cp(view("bkl"), view("bki"))
    cp(view("qcl"), view("qci"))
    ts(view("qsf"), view("qsi"), 1.0 / 16384, OP.mult)
    act(view("lrow"), view("io640"), idx=view("qcl"))
    ts(view("lm"), view("lrow"), A_, OP.is_equal)
    const(view("xk", 128, 640))
    const(view("cnt", 0, 1), 128)
    build0(0, 128)
    build(0, 2)
    iota(view("cst"), [[16, 16], [0, 8]], 1)

    def consts():
        lin(PI1, PI_, 1.0, 1.0)
        lin(A15, A_, -1.0, 15.0)
        for t in range(3):
            ts(ix(8 + t), A_, float(t), OP.not_equal)
            ts(ix(12 + t), A_, float(t), OP.is_equal)
        ts(ix(11), A_, 3.0, OP.is_ge)
        const(view("z8"))
        const(view("zb"))
        ts(view("zb", 120, 128), view("pg", 0, 8), G_, OP.is_equal)
        ts(view("blki"), view("pg"), G_, OP.is_equal)
        ts(view("blkpp"), view("pg"), PG_, OP.is_equal)
        ts(view("blkp"), view("qg"), PG_, OP.is_equal)
        ts(view("cst"), view("cst"), A_, OP.add)
        tt(view("cst"), view("cst"), view("blki"), OP.mult)
        ts(view("cst"), view("cst"), -1.0, OP.add)
        ts(view("tmp", 0, 128), view("qm"), PI1, OP.is_equal)
        tt(view("pmx"), view("tmp", 0, 128), view("blkp"), OP.mult)
        ts(view("tmp", 128, 256), view("qm"), PI1, OP.is_gt, -1.0, OP.add)
        tt(view("tmb"), view("tmp", 128, 256), view("blkp"), OP.mult)
        lin(view("npm"), view("c8"), 1.0, PI_)
        lin(view("cnp"), view("npm"), 1.0, -511.0)
        lin(view("sm", 4, 5), A_, -1.0, 639.0)
        lin(view("nlneg"), view("c8"), -1.0, view("sm", 4, 5))
        tt(view("c15"), view("eqm", 0, 16), view("c16", 16, 32), OP.mult)
        const(view("b16"), 16)
        scale(view("d15"), view("i128"), A15)
        lin(view("low"), view("blk"), 256.0, -256.0)
        tt(view("low"), view("low"), view("d15"), OP.add)
        for t in range(3):
            scale(view("keep", 128 * t, 128 * t + 128), view("i128"), ix(8 + t))
        lin(view("nj"), jj(2), -2.0)
        move(view("num", 0, 128), view("io640", 0, 128))

    xw, ow = view("xw"), view("ow")
    rot = {"g3": 0, "g4": 0}

    def buf(kind):
        k = 1024 * (rot[kind] % 8)
        rot[kind] += 1
        return view(kind, k, k + 1024)

    def pl(t):
        return view("pl", 8 * t, 8 * t + 8)

    def lookup(t):
        if t == 0:
            ts(view("ki"), view("qsf", 0, 8), 128.0, OP.mult, -EPS, OP.add)
        else:
            ts(view("ki"), view("qsf", 8 * t, 8 * t + 8), view("pd0", 8, 9), OP.mult, -EPS, OP.add)
        cp(view("kl"), view("ki"))
        if t:
            scatter(view("xk"), pl(t - 1), view("xi"))
        tt(view("qgt"), view("xk") if t else view("xk", 0, 128), view("lm", 128 * t, 128 * t + 128), OP.mult, idx=view("kl"))
        mms(view("pa0", 0, 8), [(jj(i), view("qgt", i, 128, 16)) for i in range(16)])
        ts(view("ql"), view("pa0", 0, 8), 2048.0, OP.add)

    def pass1(b):
        lst_ = view("bkl") if b == 0 else view("ql")
        ts(view("xl%d" % (b % 2)), xw, 0.0625, OP.mult, -C23, OP.add, idx=lst_)
        step(view("xk", 0, 128) if b == 0 else view("xi"), lst_)

    def pass2(b):
        for h in (0, 1):
            step(view("y%d" % b, 1024 * h, 1024 * h + 1024), view("xl%d" % (b % 2), 64 * h, 64 * h + 64))

    def psel_x(b, out):
        for h in (0, 1):
            bank = view("pa%d" % h, 0, 64)
            mms(bank, [(sel(0, 0, a), view("y%d" % b, 1024 * h + a, 1024 * h + 1024, 16)) for a in range(16)])
            ts(view(out, 64 * h, 64 * h + 64), bank, 2048.0, OP.add)

    def psel_z(b, z, n=1):
        for k in range(n):
            mms(view("pe0", 128 * k, 128 * k + 128), [(sel(0, 1 + z, a), view("y%d" % (b + k), a, 2048, 16)) for a in range(16)], 1, PARTS)
        move(view("pz%d" % z, 128 * b, 128 * b + 128 * n), view("pe0", 0, 128 * n))

    def p3(s, src, out, slow=0):
        for h in (0, 1):
            bank = view(("pa%d" % h, "pb%d" % h, "pe0")[slow], 64 * h, 64 * h + 64)
            g3 = buf("g3")
            w = 32 if slow == 2 else 64
            for a in range(0, 64, w):
                step(view("g3", g3[2] + 16 * a, g3[2] + 16 * (a + w)), view(src, 64 * h + a, 64 * h + a + w))
            mms(bank, [(sel(1, s, e), view("g3", g3[2] + e, g3[3], 16)) for e in range(16)])
            ts(view(out, 64 * h, 64 * h + 64), bank, 2048.0, OP.add)

    def p4g(h, src):
        g4 = buf("g4")
        move(g4, ow, idx=view(src, 64 * h, 64 * h + 64))
        return g4

    def p4s(h, g4, extra=(), skip=-1, s=0):
        bank = view("pb%d" % h, 0, 64)
        mms(bank, [(sel(2, s, e), view("g4", g4[2] + e, g4[3], 16)) for e in range(16) if e != skip] + list(extra))
        return bank

    def p4z(s, src, w=64):
        for a in range(0, 128, w):
            move(view("gt", 16 * a, 16 * (a + w)), ow, idx=view(src, a, a + w))
        bank, m = view("pb%d" % (s % 2), 0, 128), 128 * (s - 2)

        def fn(e):
            for k in range(16):
                r = e.matmul(T[bank[1]][:, k:128:16], T.gt[:, k:2048:16], T.st[:, m + 8 * k:m + 8 * k + 8], True, True)
            return r
        do({"P": (fn, (0, 0, 0, 16 * 64))}, [view("gt"), view("st", m, m + 128)], [bank])
        return bank

    def evac_r(b, h, bank):
        move(view("rr", 128 * b + 64 * h, 128 * b + 64 * h + 64), bank)

    def compare(t):
        b, L = t + 1, 128 * (t + 1)
        q = view("rr", 128 * b, 128 * b + 128)
        act(view("r2", 0, L), view("rr", 0, L), scale=32.0, func=AF.Square)
        act(view("rq2"), q, scale=32.0, func=AF.Square)
        for k in range(8):
            scale(view("lhb", k, 1024, 8), q, view("b8f", 8 + k, 9 + k), free=True)
        for c in range(8):
            bank = view(("pc0", "pc1", "pa1")[c % 3], 0, L)
            mms(bank, [(view("blki"), view("r2", 0, L)), (view("lhb", 128 * c, 128 * c + 128), view("rr", 0, L))])
            scan(view("sc", 384 * c, 384 * c + L), bank, view("neg1", 0, L), 8000000.0, OP.min, OP.add)
        mms(view("pd0", 0, 8), [(view("zb", 120 - 8 * i, 248 - 8 * i), view("rq2", i, 128, 16)) for i in range(16)])
        act(view("nn"), view("pd0", 0, 8), scale=-1.0)

    def append(t):
        L, b = 128 * (t + 1), t + 1
        last = (T.sc[:, L - 1::384], "sc", 0, 3072, 8)
        tt(view("uu"), last, view("nn"), OP.is_ge)
        scan(view("inc"), view("uu"), view("z8"), 0.0, OP.add, OP.add)
        tt(view("vl"), last, view("nn"), OP.subtract)
        tt(view("ww"), view("uu"), view("cnp"), OP.mult)
        mms(view("pd0", 8, 9), [(view("i128"), view("cnt", t, t + 1)), (view("blkp"), view("inc", 7, 8))])
        mms(view("pd0", 0, 8), [(view("blkp"), view("inc")), (view("tmb"), view("uu")), (view("i128"), view("nlneg")), (view("pmx"), view("ww"))])
        if t < 2:
            mms(view("pd0", 9, 10), [(view("blkpp"), view("inc", 7, 8))])
        tt(view("mn"), view("vl"), view("npm"), OP.min)
        mms(view("pc0", 0, 8), [(view("pmx"), view("mn"))])
        cp(pl(t), view("pd0", 0, 8))
        if t < 2:
            lookup(t + 1)
            move(view("cnt", t + 1, t + 2), view("pd0", 8, 9))
            ts(view("cnp"), view("cnp"), view("pd0", 9, 10), OP.add)
        ts(view("ml"), view("pc0", 0, 8), float(L), OP.add)
        nb = view("num", 128 * b, 128 * b + 128)
        move(nb, view("io640"), idx=pl(t))
        move(view("ymt", 128 * t, 128 * t + 128), view("num", 0, 128 * b + 128), idx=view("ml"))
        if t:
            ts(view("lm3"), view("pz%d" % t, 0, L + 128), 2048.0, OP.add, idx=view("ml"))
        else:
            tt(view("ne"), view("an"), view("aq"), OP.not_equal, idx=view("ml"))
        if t < 2:
            q = view("rr", 128 * b, 128 * b + 128)
            ts(view("inv"), nb, 512.0, OP.is_ge, 16.0, OP.mult)
            tt(q, q, view("inv"), OP.max)
        else:
            ts(view("invn"), view("io640", 0, 512), view("pd0", 8, 9), OP.is_ge)
            move(view("pzn", 0, 128), view("pz2", 0, 128))
            move(view("rn", 0, 128), view("rr", 0, 128))
            for k in range(3):
                scatter(view("pzn"), pl(k), view("pz2", 128 * k + 128, 128 * k + 256))
                scatter(view("rn"), pl(k), view("rr", 128 * k + 128, 128 * k + 256))

    def winner(t):
        mx = view("sm", 1, 2)
        if t:
            sc = view("pd0", 48, 49)
            mms(view("pd0", 64, 192), [(view("blk"), view("low")), (view("b16"), view("ne"))])
            mms(sc, [(view("d15"), view("jb", 0, 1)), (view("ne"), view("b16", 0, 1))])
            reduce(mx, view("pd0", 64, 192), OP.max)
        else:
            dc, sc = view("sm", 0, 1), view("sm", 2, 3)
            reduce(dc, view("ne"), OP.add)
            ts(view("dd2"), view("eqm", 0, 16), dc, OP.mult, 16.0, OP.mult)
            mms(view("pd0", 16, 32), [(view("blk"), view("dd2")), (view("blk"), view("c15"))])
            ts(sc, dc, 16.0, OP.mult, A15, OP.add)
            reduce(mx, view("pd0", 16, 32), OP.max)
        oh = view("oh", t, t + 1)
        ts(oh, sc, mx, OP.is_equal)
        scale(view("ws"), view("wdf", 4 * t + 4, 4 * t + 8), oh)
        mms(view("pd0", 32, 36), [(view("blk"), view("ws"))])
        ts(view("mk", 2 * t, 2 * t + 2), view("pd0", 34, 36), A_, OP.is_equal)
        lin(view("mk", 8 + t, 9 + t), view("mk", 2 * t, 2 * t + 1), 0.0625)
        lin(view("mk", 12 + t, 13 + t), view("mk", 2 * t, 2 * t + 1), -C23 - 2048.0)
        if t == 0:
            ts(view("mk", 15, 16), view("pd0", 32, 33), 16.0, OP.mult, view("pd0", 33, 34), OP.add)
        scale(view("ya", 4 * t, 4 * t + 4), view("pd0", 32, 36), ix(12 + t))

    def wpass(t, c0, c1, src):
        n = (c1 - c0) // 16
        h = (c1 - c0) // (2 if n > 16 else 1)
        for a in range(c0, c1, h):
            scale(view("pw", a, a + h), view(src, a, a + h), view("oh", t, t + 1))
        bank, bank2 = view("pc0", 0, n), view("pc1", 0, n)
        mms(bank, [(jj(i), view("pw", c0 + i, c1, 16)) for i in range(16)])
        lw, lw2 = view("lw", 0, n), view("lw2", 0, n)
        ts(lw, bank, 2048.0, OP.add)
        m16, mb = view("mk", 8 + t, 9 + t), view("mk", 12 + t, 13 + t)
        for a in range(0, c1 - c0, h):
            o, li = view("gw", a, a + h), view("lw", a // 16, (a + h) // 16)
            do({"S": a_act(o, xw, m16, mb, idx=li), "V": a_ts(o, xw, -C27 - 32768.0, OP.add, m16, OP.mult, idx=li)}, [xw, m16, mb, li], [o])
        mms(bank2, [(jj(i), view("gw", i, c1 - c0, 16)) for i in range(16)])
        ts(lw2, bank2, 2048.0, OP.add)
        for a in range(0, c1 - c0, h):
            scale(view("gz%d" % t, c0 + a, c0 + a + h), ow, view("mk", 2 * t + 1, 2 * t + 2), idx=view("lw2", a // 16, (a + h) // 16))

    def rupdate(t):
        L = 128 * (t + 2)
        bank = view("pc0", 0, L)
        mms(bank, [(view("keep", 128 * t, 128 * t + 128), view("rr", 0, L)), (jj(t), view("gz%d" % t, 0, L))])
        move(view("rr", 0, L), bank)

    pass1(0)
    lookup(0)
    pass1(1)
    pass2(0)
    psel_x(0, "l30")
    pass2(1)
    psel_x(1, "l31")
    p3(0, "l30", "l40")
    p3(0, "l31", "l41")
    build0(1, 384)
    for b in (0, 1):
        for h in (0, 1):
            evac_r(b, h, p4s(h, p4g(h, "l4%d" % b)))
    consts()
    build(2, BLOCKS)
    buildS()
    for z in range(3):
        psel_z(0, z, 2)
    compare(0)
    for b, x in ((1, 2), (0, 3)):
        ts(view("l3%d" % x), view("pz0", 128 * b, 128 * b + 128), 2048.0, OP.add)
        p3(1, "l3%d" % x, "l4%d" % (x if x == 2 else 4), 1)
        for h in (0, 1):
            c = 128 * b + 64 * h
            move(view("an", c, c + 64), p4s(h, p4g(h, "l4%d" % (x if x == 2 else 4)), s=1))
    move(view("aq"), view("an", 128, 256))
    for t in range(3):
        b = t + 2
        append(t)
        if t:
            p3(1 + t, "lm3", "l43")
        if t < 2:
            pass1(b)
            pass2(b)
            psel_x(b, "l31")
        if t:
            tt(view("ne"), p4z(1 + t, "l43"), view("aq"), OP.not_equal)
        winner(t)
        if t < 2:
            for z in range(t, 2):
                psel_z(b, z)
            p3(0, "l31", "l41")
        if t == 0:
            scale(view("gz0", 0, 256), view("an"), view("oh", 0, 1))
            wpass(0, 256, 384, "pz0")
        else:
            wpass(t, 0, 512, "pzn" if t == 2 else "pz1")
        if t == 2:
            break
        gs = [p4g(h, "l41") for h in (0, 1)]
        rupdate(t)
        for h in (0, 1):
            c = 128 * b + 64 * h
            evac_r(b, h, p4s(h, gs[h], [(jj(t), view("gz%d" % t, c, c + 64))], t))
        if t == 0:
            ts(view("sel", 0, 2048, 16), view("cst"), view("mk", 15, 16), OP.is_equal)
            for k in (1, 2):
                ts(view("sel", block(k, 0), block(k, 0) + 128, 16), view("b8f", 0, 8), view("mk", k - 1, k), OP.mult)
        psel_z(b, 2)
        compare(t + 1)
        ts(view("l32"), view("pz%d" % (t + 1), 128 * b, 128 * b + 128), 2048.0, OP.add)
        p3(2 + t, "l32", "l42", 2)
        move(view("aq"), p4z(2 + t, "l42", 32))

    ends = []

    def out(dst_ap, src_ap, v, sem):
        do({"Y": (lambda e: e.dma_start(dst_ap, src_ap).then_inc(T.sem[sem], 16), (0.1, 0, 0, 0))}, [v], [], lat=2.0, tok=())
        ends.append(sem)
    out(T.ym[:], T.ymt[::16, :], view("ymt"), "dym")
    yet = view("ya", 12, 16)
    scale(yet, view("wdf", 0, 4), ix(11))
    for t in range(3):
        tt(yet, yet, view("ya", 4 * t, 4 * t + 4), OP.add)
    out(T.ye[:], T.ya[:, 12:16], yet, "dye")
    mms(view("pc0"), [(view("keep", 256, 384), view("rn", 0, 512)), (view("nj"), view("invn")), (jj(2), view("gz2"))])
    ts(view("yrt"), view("pc0"), -1.0, OP.max)
    out(T.yr[:], T.yrt[:], view("yrt"), "dyr")

    PLAN["ops"], PLAN["p"] = ops, plan(ops)
    pos = {q: 0 for q in queue}
    seen = {q: {} for q in queue}
    for i, q in PLAN["p"]:
        ops[i]["run"] = q
    for i, q in PLAN["p"]:
        o = ops[i]
        if q == "D":
            continue
        want = {}
        for d in o["deps"] | set(d for d in o["soft"] if ops[d]["run"] != q):
            if ops[d]["tok"]:
                s, n = ops[d]["tok"]
                want[s] = max(want.get(s, 0), n)
        for s in sorted(want):
            if seen[q].get(s, 0) < want[s]:
                queue[q].wait_ge(T.sem[s], want[s])
                seen[q][s] = want[s]
        r = o["alt"][q][0](queue[q])
        if o["tok"] is None:
            pos[q] += 1
            r.then_inc(T.sem[CSEM[q]], 1)
            o["tok"] = (CSEM[q], pos[q])
    for s in ends:
        g.sync.wait_ge(T.sem[s], 16)
    g.wait_ge(T.sem.sent, (NCH + len(OWS)) * neng)
    for q in sorted(CSEM):
        g.wait_ge(T.sem[CSEM[q]], pos[q])
